import numpy as np
import ml_dtypes


def mxq(x, axis, fmt="e4m3"):
    dtype, down = {"e4m3": (ml_dtypes.float8_e4m3fn, 7), "e5m2": (ml_dtypes.float8_e5m2, 14)}[fmt]
    v = np.moveaxis(np.asarray(x, np.float32).astype(ml_dtypes.bfloat16).astype(np.float64), axis, -1)
    blocks = v.reshape(v.shape[:-1] + (-1, 32))
    amax = np.abs(blocks).max(-1, keepdims=True)
    byte = np.maximum(np.where(amax > 0, np.frexp(amax)[1] - 1 + 127, 0) - down, 1)
    scale = np.exp2(byte - 127.0)
    codes = (blocks / scale).astype(np.float32).astype(dtype).astype(np.float64)
    return np.moveaxis((codes * scale).reshape(v.shape), -1, axis)


WIDE = False


def mx_kscale(k):
    if not WIDE:
        return np.ones(k)
    levels = np.array([10, -10, 5, -5, 0])
    if k % 512:
        return np.exp2(np.random.permutation(np.resize(levels, k // 32))).repeat(32)
    a = np.empty((k // 512, 16))
    for p in range(k // 512):
        a[p, :8] = np.random.permutation(np.resize(levels, 8))
        for g in range(8):
            far = levels[np.abs(levels - a[p, g]) >= 10]
            a[p, g + 8] = far[np.random.randint(len(far))]
    return np.exp2(a.ravel()).repeat(32)


def f64(x):
    return np.asarray(x).astype(np.float64)


def striped(idx):
    return np.tile(idx.reshape(-1, 16).T, (8, 1)).astype(np.uint16)


def unstriped(offs):
    return offs[:16].T.reshape(-1).astype(np.int64)


E2M1 = np.array([0.0, 0.5, 1.0, 1.5, 2.0, 3.0, 4.0, 6.0, -0.0, -0.5, -1.0, -1.5, -2.0, -3.0, -4.0, -6.0])


def pack_fp4(w):
    k, n = w.shape
    w = f64(np.asarray(w, np.float32).astype(ml_dtypes.bfloat16)).reshape(k // 32, 32, n)
    amax = np.abs(w).max(1)
    mant, ex = np.frexp(amax / 6.0)
    byte = np.clip(np.where(amax > 0, np.where(mant > 0.5, ex, ex - 1) + 127, 1), 1, 254)
    scaled = (w * np.exp2(127.0 - byte)[:, None, :]).reshape(k, n).astype(np.float32)
    c = np.ascontiguousarray(scaled.reshape(k // 512, 128, 4, n).transpose(0, 1, 3, 2)).astype(ml_dtypes.float4_e2m1fn).view(np.uint8) & 0xF
    words = (c[..., 0::2] | (c[..., 1::2] << 4)).reshape(k // 512, 128, 2 * n)
    return np.ascontiguousarray(words), np.ascontiguousarray(byte.astype(np.uint8).reshape(k // 512, 16, n))


def unpack_fp4(words, scales):
    g, _, n = scales.shape
    words = np.ascontiguousarray(words).reshape(g, 128, n, 2)
    nib = np.empty((g, 128, n, 4), np.uint8)
    nib[..., 0::2] = words & 0xF
    nib[..., 1::2] = words >> 4
    vals = E2M1[nib] * np.repeat(np.exp2(scales.astype(np.float64) - 127.0), 8, axis=1)[..., None]
    return vals.transpose(0, 1, 3, 2).reshape(g * 512, n)


def silu(v):
    return v / (1.0 + np.exp(-np.maximum(v, -700.0)))


K, T, S, V, H, N, J = 512, 2048, 1024, 512, 512, 256, 512


def setup_inputs():
    n = np.random.standard_normal
    s = mx_kscale(K)[:, None]
    u = mx_kscale(H)
    r = mx_kscale(J)[:, None]
    packed_w4 = pack_fp4(n((H, N)) / np.sqrt(H) / u[:, None])
    return {
        "xT": (n((K, T)) * s).astype(np.float32),
        "eT": (n((J, V)) * r).astype(np.float32),
        "w1": (n((K, H)) / np.sqrt(3 * K) / s * u).astype(np.float32),
        "w2": (n((K, H)) / np.sqrt(3 * K) / s * u).astype(np.float32),
        "w3": (n((J, H)) / np.sqrt(3 * J) / r * u).astype(np.float32),
        "w4_words": packed_w4[0],
        "w4_scales": packed_w4[1],
        "offs": striped(np.random.permutation(T)[:S]),
    }


def reference(xT, eT, w1, w2, w3, w4_words, w4_scales, offs):
    xq = mxq(f64(xT)[:, unstriped(offs)], 0, "e4m3")
    h = silu(mxq(f64(w1), 0, "e4m3").T @ xq[:, :V] + mxq(f64(w2), 0, "e4m3").T @ xq[:, V:2 * V] + mxq(f64(w3), 0, "e4m3").T @ mxq(f64(eT), 0, "e4m3"))
    return unpack_fp4(w4_words, w4_scales).T @ mxq(h, 0, "e4m3")

@@ -1,0 +1,161 @@
+from contextlib import ExitStack
+
+import concourse.mybir as mybir
+
+K, T, S, V, H, N = 512, 2048, 1024, 512, 512, 256
+FLOPS = 2 * V * (3 * K * H + H * N)
+
+F32 = mybir.dt.float32
+BF16 = mybir.dt.bfloat16
+U32 = mybir.dt.uint32
+I32 = mybir.dt.int32
+U16 = mybir.dt.uint16
+U8 = mybir.dt.uint8
+FP8X4 = mybir.dt.float8_e4m3fn_x4
+FP4X4 = mybir.dt.float4_e2m1fn_x4
+SILU = mybir.ActivationFunctionType.Silu
+
+P = 128
+PACK = 4
+BLOCK = 128
+BLOCKS = V // BLOCK
+
+
+def tile_picked_edgeup_silu_e_kernel(tc, xT, eT, w1, w2, w3, w4_words, w4_scales, offs, out):
+    nc = tc.nc
+    with ExitStack() as ctx:
+        keep = ctx.enter_context(tc.tile_pool(name="keep", bufs=1))
+        psum = ctx.enter_context(tc.psum_pool(name="psum", bufs=1))
+
+        def quantize(name, values, width):
+            codes = keep.tile([P, width], U32, name=name + "_codes", align_bytes=64)
+            scales = keep.tile([P, width], U8, name=name + "_scales", align_bytes=64)
+            nc.vector.quantize_mx(out=codes[:].bitcast(FP8X4), scales=scales[:], in_=values)
+            return codes, scales
+
+        zero = keep.tile([P, 1], F32, name="zero")
+        nc.vector.memset(zero[:], 0.0)
+        bias = keep.tile([P, 1], F32, name="bias")
+        nc.scalar.activation(bias[:], zero[:], SILU)
+        w4_s = keep.tile([P, N], U8, name="w4_s", align_bytes=64)
+        nc.vector.memset(w4_s[:].bitcast(I32), 0)
+
+        x_rows = xT.rearrange("(p j) t -> p j t", j=PACK)
+        x_chunks = [(0, 0, 1024, 0), (0, 1024, 2048, 672), (1, 0, 1024, 0), (1, 1024, 1536, 512), (1, 1536, 2048, 336)]
+        x_raw = []
+        offsets = keep.tile([P, S // 16], U16, name="offsets")
+        for i, (u, c0, c1, share) in enumerate(x_chunks):
+            raw = keep.tile([P, 2, c1 - c0], F32, name="x_raw%d" % i)
+            nc.sync.dma_start(out=raw[:], in_=x_rows[:, 2 * u : 2 * u + 2, c0:c1])
+            x_raw.append(raw)
+            if i == 0:
+                nc.sync.dma_start(offsets[:], offs)
+        w_raw = []
+        for i, w in enumerate((w1, w2, w3)):
+            raw = keep.tile([P, PACK, H], F32, name="w_raw%d" % i)
+            nc.sync.dma_start(out=raw[:], in_=w.rearrange("(p j) c -> p j c", j=PACK))
+            w_raw.append(raw)
+        e_rows = eT.rearrange("(p j) v -> p j v", j=PACK)
+        e_raw = []
+        for i in range(2):
+            raw = keep.tile([P, PACK, 256], F32, name="e_raw%d" % i)
+            nc.sync.dma_start(out=raw[:], in_=e_rows[:, :, 256 * i : 256 * (i + 1)])
+            e_raw.append(raw)
+        w4_w = keep.tile([P, 2 * N], U8, name="w4_w", align_bytes=64)
+        nc.sync.dma_start(out=w4_w[:], in_=w4_words[0])
+        for q in range(4):
+            nc.sync.dma_start(out=w4_s[32 * q : 32 * q + 4, :].bitcast(I32), in_=w4_scales[0, 4 * q : 4 * q + 4, :].bitcast(I32))
+
+        pairs = [keep.tile([P, T], U32, name="pairs%d" % u, align_bytes=64) for u in range(2)]
+        picked = [keep.tile([P, V * PACK], BF16, name="picked%d" % s, align_bytes=64) for s in range(2)]
+
+        def cast_pairs(i):
+            u, c0, c1, share = x_chunks[i]
+            dst = pairs[u][:].bitcast(BF16).rearrange("p (c i e) -> p c e i", i=4, e=2)
+            src = x_raw[i][:].rearrange("p e (c i) -> p c e i", i=4)
+            n, a, b = (c1 - c0) // 4, share // 4, c0 // 4
+            if a > 0:
+                nc.vector.tensor_copy(out=dst[:, b : b + a], in_=src[:, 0:a])
+            if a < n:
+                nc.scalar.copy(out=dst[:, b + a : b + n], in_=src[:, a:n])
+
+        def gather(u, s):
+            dst = picked[s][:].bitcast(U32).rearrange("p (v u) -> p v u", u=2)[:, :, u]
+            nc.vector.tensor_copy(out=dst, in_=pairs[u][:].indirect(offsets[:, 32 * s : 32 * (s + 1)]))
+
+        cast_pairs(0)
+        cast_pairs(1)
+        gather(0, 0)
+        gather(0, 1)
+        cast_pairs(2)
+        cast_pairs(3)
+        cast_pairs(4)
+        gather(1, 0)
+        gather(1, 1)
+        x_q = [quantize("x%d" % s, picked[s][:], V) for s in range(2)]
+
+        w_q = []
+        w_share = [0, 64, 84]
+        for i in range(3):
+            grouped = keep.tile([P, PACK * H], BF16, name="w_bf%d" % i, align_bytes=64)
+            dst = grouped[:].rearrange("p (t m j) -> p m j t", t=PACK, j=PACK)
+            src = w_raw[i][:].rearrange("p j (m t) -> p m j t", t=PACK)
+            a = w_share[i]
+            if a > 0:
+                nc.vector.tensor_copy(out=dst[:, 0:a], in_=src[:, 0:a])
+            nc.scalar.copy(out=dst[:, a:P], in_=src[:, a:P])
+            if i < 2:
+                w_q.append([quantize("w%d" % i, grouped[:], H)])
+            else:
+                w_q.append([quantize("w%d_%d" % (i, g), grouped[:, 1024 * g : 1024 * (g + 1)], 256) for g in range(2)])
+
+        def w_tile(i, t):
+            per = PACK // len(w_q[i])
+            codes, scales = w_q[i][t // per]
+            cols = slice((t % per) * P, (t % per + 1) * P)
+            return codes[:, cols].bitcast(FP8X4), scales[:, cols]
+
+        acc = [psum.tile([P, PACK, BLOCK], F32, name="acc%d" % b) for b in range(BLOCKS)]
+        def x_passes(i, b):
+            for t in range(PACK):
+                cols = slice(b * BLOCK, (b + 1) * BLOCK)
+                wc, ws = w_tile(i, t)
+                nc.tensor.matmul_mx(out=acc[b][:, t, :], lhsT=wc, lhsT_scale=ws,
+                                    rhs=x_q[i][0][:, cols].bitcast(FP8X4), rhs_scale=x_q[i][1][:, cols],
+                                    start=(i == 0 and t == 0), stop=False)
+
+        for b in range(BLOCKS):
+            x_passes(0, b)
+
+        e_q = []
+        for b in range(2):
+            e_bf = keep.tile([P, BLOCK * PACK], BF16, name="e_bf%d" % b, align_bytes=64)
+            src = e_raw[0][:, :, b * BLOCK : (b + 1) * BLOCK].rearrange("p j (c i) -> p c j i", i=4)
+            nc.scalar.copy(out=e_bf[:].rearrange("p (c i j) -> p c j i", i=4, j=PACK), in_=src)
+            ec, es = quantize("e%d" % b, e_bf[:], BLOCK)
+            e_q.append((ec[:], es[:]))
+        e_bf = keep.tile([P, 2 * BLOCK * PACK], BF16, name="e_bf2", align_bytes=64)
+        nc.vector.tensor_copy(out=e_bf[:].rearrange("p (c i j) -> p c j i", i=4, j=PACK), in_=e_raw[1][:].rearrange("p j (c i) -> p c j i", i=4))
+        ec, es = quantize("e2", e_bf[:], 2 * BLOCK)
+        for b in range(2):
+            e_q.append((ec[:, b * BLOCK : (b + 1) * BLOCK], es[:, b * BLOCK : (b + 1) * BLOCK]))
+
+        out_rows = out.rearrange("(g p) v -> p g v", p=P)
+        for b in range(BLOCKS):
+            x_passes(1, b)
+            for t in range(PACK):
+                wc, ws = w_tile(2, t)
+                nc.tensor.matmul_mx(out=acc[b][:, t, :], lhsT=wc, lhsT_scale=ws,
+                                    rhs=e_q[b][0].bitcast(FP8X4), rhs_scale=e_q[b][1],
+                                    start=False, stop=(t == PACK - 1))
+            h_bf = keep.tile([P, BLOCK * PACK], BF16, name="h_bf%d" % b, align_bytes=64)
+            nc.scalar.activation(h_bf[:].rearrange("p (v t) -> p v t", t=PACK), acc[b][:].rearrange("p t v -> p v t"), SILU, bias=bias[:])
+            hc, hs = quantize("h%d" % b, h_bf[:], BLOCK)
+            res = psum.tile([P, 2, BLOCK], F32, name="res%d" % b)
+            for g in range(2):
+                nc.tensor.matmul_mx(out=res[:, g, :], lhsT=w4_w[:, 2 * P * g : 2 * P * (g + 1)].bitcast(FP4X4),
+                                    lhsT_scale=w4_s[:, P * g : P * (g + 1)],
+                                    rhs=hc[:].bitcast(FP8X4), rhs_scale=hs[:], start=True, stop=True)
+            res_sb = keep.tile([P, 2, BLOCK], F32, name="res_sb%d" % b)
+            nc.vector.tensor_copy(out=res_sb[:], in_=res[:])
+            nc.sync.dma_start(out=out_rows[:, :, b * BLOCK : (b + 1) * BLOCK], in_=res_sb[:])

@@ -27,8 +27,8 @@ def tile_picked_edgeup_silu_e_kernel(tc, xT, eT, w1, w2, w3, w4_words, w4_scales
         keep = ctx.enter_context(tc.tile_pool(name="keep", bufs=1))
         psum = ctx.enter_context(tc.psum_pool(name="psum", bufs=1))
 
-        def quantize(name, values, width):
-            codes = keep.tile([P, width], U32, name=name + "_codes", align_bytes=64)
+        def quantize(name, values, width, tag=None):
+            codes = keep.tile([P, width], U32, name=name + "_codes", tag=tag or name + "_codes", align_bytes=64)
             scales = keep.tile([P, width], U8, name=name + "_scales", align_bytes=64)
             nc.vector.quantize_mx(out=codes[:].bitcast(FP8X4), scales=scales[:], in_=values)
             return codes, scales
@@ -64,7 +64,7 @@ def tile_picked_edgeup_silu_e_kernel(tc, xT, eT, w1, w2, w3, w4_words, w4_scales
         w4_w = keep.tile([P, 2 * N], U8, name="w4_w", align_bytes=64)
         nc.sync.dma_start(out=w4_w[:], in_=w4_words[0])
         for q in range(4):
-            nc.sync.dma_start(out=w4_s[32 * q : 32 * q + 4, :].bitcast(I32), in_=w4_scales[0, 4 * q : 4 * q + 4, :].bitcast(I32))
+            nc.gpsimd.dma_start(out=w4_s[32 * q : 32 * q + 4, :].bitcast(I32), in_=w4_scales[0, 4 * q : 4 * q + 4, :].bitcast(I32))
 
         pairs = [keep.tile([P, T], U32, name="pairs%d" % u, align_bytes=64) for u in range(2)]
         picked = [keep.tile([P, V * PACK], BF16, name="picked%d" % s, align_bytes=64) for s in range(2)]
@@ -92,11 +92,19 @@ def tile_picked_edgeup_silu_e_kernel(tc, xT, eT, w1, w2, w3, w4_words, w4_scales
         cast_pairs(4)
         gather(1, 0)
         gather(1, 1)
-        x_q = [quantize("x%d" % s, picked[s][:], V) for s in range(2)]
+        x_q = [quantize("x0", picked[0][:], V)]
+        w1_q = []
+        for g in range(2):
+            half = keep.tile([P, 2 * H], BF16, name="w1_bf%d" % g, tag="w1_bf%d" % g, align_bytes=64)
+            nc.scalar.copy(out=half[:].rearrange("p (t m j) -> p m j t", t=2, j=PACK),
+                           in_=w_raw[0][:].rearrange("p j (m t) -> p m j t", t=PACK)[:, :, :, 2 * g : 2 * g + 2])
+            w1_q.append(quantize("w0_%d" % g, half[:], 256))
+            if g == 0:
+                x_q.append(quantize("x1", picked[1][:], V, tag="w1_bf0"))
 
-        w_q = []
+        w_q = [w1_q]
         w_share = [0, 64, 84]
-        for i in range(3):
+        for i in range(1, 3):
             grouped = keep.tile([P, PACK * H], BF16, name="w_bf%d" % i, align_bytes=64)
             dst = grouped[:].rearrange("p (t m j) -> p m j t", t=PACK, j=PACK)
             src = w_raw[i][:].rearrange("p j (m t) -> p m j t", t=PACK)
@@ -116,33 +124,36 @@ def tile_picked_edgeup_silu_e_kernel(tc, xT, eT, w1, w2, w3, w4_words, w4_scales
             return codes[:, cols].bitcast(FP8X4), scales[:, cols]
 
         acc = [psum.tile([P, PACK, BLOCK], F32, name="acc%d" % b) for b in range(BLOCKS)]
-        def x_passes(i, b):
-            for t in range(PACK):
+        def x_passes(i, b, ts):
+            for t in ts:
                 cols = slice(b * BLOCK, (b + 1) * BLOCK)
                 wc, ws = w_tile(i, t)
                 nc.tensor.matmul_mx(out=acc[b][:, t, :], lhsT=wc, lhsT_scale=ws,
                                     rhs=x_q[i][0][:, cols].bitcast(FP8X4), rhs_scale=x_q[i][1][:, cols],
                                     start=(i == 0 and t == 0), stop=False)
 
-        for b in range(BLOCKS):
-            x_passes(0, b)
+        for g in range(2):
+            for b in range(BLOCKS):
+                x_passes(0, b, (2 * g, 2 * g + 1))
 
         e_q = []
-        for b in range(2):
-            e_bf = keep.tile([P, BLOCK * PACK], BF16, name="e_bf%d" % b, align_bytes=64)
-            src = e_raw[0][:, :, b * BLOCK : (b + 1) * BLOCK].rearrange("p j (c i) -> p c j i", i=4)
-            nc.scalar.copy(out=e_bf[:].rearrange("p (c i j) -> p c j i", i=4, j=PACK), in_=src)
-            ec, es = quantize("e%d" % b, e_bf[:], BLOCK)
+        e_bf = []
+        for b in range(BLOCKS):
+            grouped = keep.tile([P, BLOCK * PACK], BF16, name="e_bf%d" % b, align_bytes=64)
+            dst = grouped[:].rearrange("p (c i j) -> p c j i", i=4, j=PACK)
+            src = e_raw[b // 2][:, :, (b % 2) * BLOCK : (b % 2 + 1) * BLOCK].rearrange("p j (c i) -> p c j i", i=4)
+            if b < 2:
+                nc.scalar.copy(out=dst, in_=src)
+            else:
+                nc.vector.tensor_copy(out=dst, in_=src)
+            e_bf.append(grouped)
+        for b in range(BLOCKS):
+            ec, es = quantize("e%d" % b, e_bf[b][:], BLOCK)
             e_q.append((ec[:], es[:]))
-        e_bf = keep.tile([P, 2 * BLOCK * PACK], BF16, name="e_bf2", align_bytes=64)
-        nc.vector.tensor_copy(out=e_bf[:].rearrange("p (c i j) -> p c j i", i=4, j=PACK), in_=e_raw[1][:].rearrange("p j (c i) -> p c j i", i=4))
-        ec, es = quantize("e2", e_bf[:], 2 * BLOCK)
-        for b in range(2):
-            e_q.append((ec[:, b * BLOCK : (b + 1) * BLOCK], es[:, b * BLOCK : (b + 1) * BLOCK]))
 
         out_rows = out.rearrange("(g p) v -> p g v", p=P)
         for b in range(BLOCKS):
-            x_passes(1, b)
+            x_passes(1, b, range(PACK))
             for t in range(PACK):
                 wc, ws = w_tile(2, t)
                 nc.tensor.matmul_mx(out=acc[b][:, t, :], lhsT=wc, lhsT_scale=ws,
@@ -151,11 +162,20 @@ def tile_picked_edgeup_silu_e_kernel(tc, xT, eT, w1, w2, w3, w4_words, w4_scales
             h_bf = keep.tile([P, BLOCK * PACK], BF16, name="h_bf%d" % b, align_bytes=64)
             nc.scalar.activation(h_bf[:].rearrange("p (v t) -> p v t", t=PACK), acc[b][:].rearrange("p t v -> p v t"), SILU, bias=bias[:])
             hc, hs = quantize("h%d" % b, h_bf[:], BLOCK)
+            last = b == BLOCKS - 1
             res = psum.tile([P, 2, BLOCK], F32, name="res%d" % b)
+            halves = [res[:, 0, :], res[:, 1, :]]
+            if last:
+                other = psum.tile([P, BLOCK], F32, name="res_other", tag="acc0")
+                halves[1] = other[:]
             for g in range(2):
-                nc.tensor.matmul_mx(out=res[:, g, :], lhsT=w4_w[:, 2 * P * g : 2 * P * (g + 1)].bitcast(FP4X4),
+                nc.tensor.matmul_mx(out=halves[g], lhsT=w4_w[:, 2 * P * g : 2 * P * (g + 1)].bitcast(FP4X4),
                                     lhsT_scale=w4_s[:, P * g : P * (g + 1)],
                                     rhs=hc[:].bitcast(FP8X4), rhs_scale=hs[:], start=True, stop=True)
             res_sb = keep.tile([P, 2, BLOCK], F32, name="res_sb%d" % b)
-            nc.vector.tensor_copy(out=res_sb[:], in_=res[:])
+            if last:
+                nc.vector.tensor_copy(out=res_sb[:, 0, :], in_=halves[0])
+                nc.scalar.copy(out=res_sb[:, 1, :], in_=halves[1])
+            else:
+                nc.vector.tensor_copy(out=res_sb[:], in_=res[:])
             nc.sync.dma_start(out=out_rows[:, :, b * BLOCK : (b + 1) * BLOCK], in_=res_sb[:])

@@ -103,19 +103,18 @@ def tile_picked_edgeup_silu_e_kernel(tc, xT, eT, w1, w2, w3, w4_words, w4_scales
                 x_q.append(quantize("x1", picked[1][:], V, tag="w1_bf0"))
 
         w_q = [w1_q]
-        w_share = [0, 64, 84]
         for i in range(1, 3):
-            grouped = keep.tile([P, PACK * H], BF16, name="w_bf%d" % i, align_bytes=64)
-            dst = grouped[:].rearrange("p (t m j) -> p m j t", t=PACK, j=PACK)
-            src = w_raw[i][:].rearrange("p j (m t) -> p m j t", t=PACK)
-            a = w_share[i]
-            if a > 0:
-                nc.vector.tensor_copy(out=dst[:, 0:a], in_=src[:, 0:a])
-            nc.scalar.copy(out=dst[:, a:P], in_=src[:, a:P])
-            if i < 2:
-                w_q.append([quantize("w%d" % i, grouped[:], H)])
-            else:
-                w_q.append([quantize("w%d_%d" % (i, g), grouped[:, 1024 * g : 1024 * (g + 1)], 256) for g in range(2)])
+            halves_bf = []
+            for g in range(2):
+                half = keep.tile([P, 2 * H], BF16, name="w%d_bf%d" % (i + 1, g), align_bytes=64)
+                dst = half[:].rearrange("p (t m j) -> p m j t", t=2, j=PACK)
+                src = w_raw[i][:].rearrange("p j (m t) -> p m j t", t=PACK)[:, :, :, 2 * g : 2 * g + 2]
+                if g == 0:
+                    nc.vector.tensor_copy(out=dst, in_=src)
+                else:
+                    nc.scalar.copy(out=dst, in_=src)
+                halves_bf.append(half)
+            w_q.append([quantize("w%d_%d" % (i, g), halves_bf[g][:], 256) for g in range(2)])
 
         def w_tile(i, t):
             per = PACK // len(w_q[i])

@@ -19,6 +19,11 @@ P = 128
 PACK = 4
 BLOCK = 128
 BLOCKS = V // BLOCK
+X_LOADS = ((0, 0, 1024, 0), (0, 1024, 2048, 672), (1, 0, 1024, 0), (1, 1024, 1536, 512), (1, 1536, 1792, 256), (1, 1792, 2048, 176))
+W_LOADS = (((0, 64, 0), (64, 128, 0)), ((0, 64, 0), (64, 128, 0)), ((0, 64, 32), (64, 128, 44)))
+W_QUANT = (1, 1, 2)
+E_LOADS = ((0, 1), (1, 2), (2, 3), (3, 4))
+E_ON_SCALAR = (128, 128, 0, 0)
 
 
 def tile_picked_edgeup_silu_e_kernel(tc, xT, eT, w1, w2, w3, w4_words, w4_scales, offs, out):
@@ -33,6 +38,12 @@ def tile_picked_edgeup_silu_e_kernel(tc, xT, eT, w1, w2, w3, w4_words, w4_scales
             nc.vector.quantize_mx(out=codes[:].bitcast(FP8X4), scales=scales[:], in_=values)
             return codes, scales
 
+        def shared_copy(dst, src, share):
+            if share > 0:
+                nc.vector.tensor_copy(out=dst[:, 0:share], in_=src[:, 0:share])
+            if share < dst.shape[1]:
+                nc.scalar.copy(out=dst[:, share:], in_=src[:, share:])
+
         zero = keep.tile([P, 1], F32, name="zero")
         nc.vector.memset(zero[:], 0.0)
         bias = keep.tile([P, 1], F32, name="bias")
@@ -41,10 +52,9 @@ def tile_picked_edgeup_silu_e_kernel(tc, xT, eT, w1, w2, w3, w4_words, w4_scales
         nc.vector.memset(w4_s[:].bitcast(I32), 0)
 
         x_rows = xT.rearrange("(p j) t -> p j t", j=PACK)
-        x_chunks = [(0, 0, 1024, 0), (0, 1024, 2048, 672), (1, 0, 1024, 0), (1, 1024, 1536, 512), (1, 1536, 2048, 336)]
         x_raw = []
         offsets = keep.tile([P, S // 16], U16, name="offsets")
-        for i, (u, c0, c1, share) in enumerate(x_chunks):
+        for i, (u, c0, c1, share) in enumerate(X_LOADS):
             raw = keep.tile([P, 2, c1 - c0], F32, name="x_raw%d" % i)
             nc.sync.dma_start(out=raw[:], in_=x_rows[:, 2 * u : 2 * u + 2, c0:c1])
             x_raw.append(raw)
@@ -52,15 +62,20 @@ def tile_picked_edgeup_silu_e_kernel(tc, xT, eT, w1, w2, w3, w4_words, w4_scales
                 nc.sync.dma_start(offsets[:], offs)
         w_raw = []
         for i, w in enumerate((w1, w2, w3)):
-            raw = keep.tile([P, PACK, H], F32, name="w_raw%d" % i)
-            nc.sync.dma_start(out=raw[:], in_=w.rearrange("(p j) c -> p j c", j=PACK))
-            w_raw.append(raw)
+            w_rows = w.rearrange("(p j) c -> p j c", j=PACK)
+            parts = []
+            for m0, m1, share in W_LOADS[i]:
+                raw = keep.tile([P, PACK, PACK * (m1 - m0)], F32, name="w_raw%d_%d" % (i, m0))
+                nc.sync.dma_start(out=raw[:], in_=w_rows[:, :, PACK * m0 : PACK * m1])
+                parts.append(raw)
+            w_raw.append(parts)
         e_rows = eT.rearrange("(p j) v -> p j v", j=PACK)
         e_raw = []
-        for i in range(2):
-            raw = keep.tile([P, PACK, 256], F32, name="e_raw%d" % i)
-            nc.sync.dma_start(out=raw[:], in_=e_rows[:, :, 256 * i : 256 * (i + 1)])
-            e_raw.append(raw)
+        for b0, b1 in E_LOADS:
+            raw = keep.tile([P, PACK, BLOCK * (b1 - b0)], F32, name="e_raw%d" % b0)
+            nc.sync.dma_start(out=raw[:], in_=e_rows[:, :, BLOCK * b0 : BLOCK * b1])
+            for b in range(b0, b1):
+                e_raw.append(raw[:, :, BLOCK * (b - b0) : BLOCK * (b - b0 + 1)])
         w4_w = keep.tile([P, 2 * N], U8, name="w4_w", align_bytes=64)
         nc.sync.dma_start(out=w4_w[:], in_=w4_words[0])
         for q in range(4):
@@ -68,53 +83,26 @@ def tile_picked_edgeup_silu_e_kernel(tc, xT, eT, w1, w2, w3, w4_words, w4_scales
 
         pairs = [keep.tile([P, T], U32, name="pairs%d" % u, align_bytes=64) for u in range(2)]
         picked = [keep.tile([P, V * PACK], BF16, name="picked%d" % s, align_bytes=64) for s in range(2)]
-
-        def cast_pairs(i):
-            u, c0, c1, share = x_chunks[i]
-            dst = pairs[u][:].bitcast(BF16).rearrange("p (c i e) -> p c e i", i=4, e=2)
-            src = x_raw[i][:].rearrange("p e (c i) -> p c e i", i=4)
-            n, a, b = (c1 - c0) // 4, share // 4, c0 // 4
-            if a > 0:
-                nc.vector.tensor_copy(out=dst[:, b : b + a], in_=src[:, 0:a])
-            if a < n:
-                nc.scalar.copy(out=dst[:, b + a : b + n], in_=src[:, a:n])
-
-        def gather(u, s):
-            dst = picked[s][:].bitcast(U32).rearrange("p (v u) -> p v u", u=2)[:, :, u]
-            nc.vector.tensor_copy(out=dst, in_=pairs[u][:].indirect(offsets[:, 32 * s : 32 * (s + 1)]))
-
-        cast_pairs(0)
-        cast_pairs(1)
-        gather(0, 0)
-        gather(0, 1)
-        cast_pairs(2)
-        cast_pairs(3)
-        cast_pairs(4)
-        gather(1, 0)
-        gather(1, 1)
+        for u in range(2):
+            for i, (uu, c0, c1, share) in enumerate(X_LOADS):
+                if uu == u:
+                    dst = pairs[u][:].bitcast(BF16).rearrange("p (c i e) -> p c e i", i=4, e=2)
+                    shared_copy(dst[:, c0 // 4 : c1 // 4], x_raw[i][:].rearrange("p e (c i) -> p c e i", i=4), share // 4)
+            for s in range(2):
+                dst = picked[s][:].bitcast(U32).rearrange("p (v u) -> p v u", u=2)[:, :, u]
+                nc.vector.tensor_copy(out=dst, in_=pairs[u][:].indirect(offsets[:, 32 * s : 32 * (s + 1)]))
         x_q = [quantize("x0", picked[0][:], V)]
-        w1_q = []
-        for g in range(2):
-            half = keep.tile([P, 2 * H], BF16, name="w1_bf%d" % g, tag="w1_bf%d" % g, align_bytes=64)
-            nc.scalar.copy(out=half[:].rearrange("p (t m j) -> p m j t", t=2, j=PACK),
-                           in_=w_raw[0][:].rearrange("p j (m t) -> p m j t", t=PACK)[:, :, :, 2 * g : 2 * g + 2])
-            w1_q.append(quantize("w0_%d" % g, half[:], 256))
-            if g == 0:
-                x_q.append(quantize("x1", picked[1][:], V, tag="w1_bf0"))
 
-        w_q = [w1_q]
-        for i in range(1, 3):
-            halves_bf = []
-            for g in range(2):
-                half = keep.tile([P, 2 * H], BF16, name="w%d_bf%d" % (i + 1, g), align_bytes=64)
-                dst = half[:].rearrange("p (t m j) -> p m j t", t=2, j=PACK)
-                src = w_raw[i][:].rearrange("p j (m t) -> p m j t", t=PACK)[:, :, :, 2 * g : 2 * g + 2]
-                if g == 0:
-                    nc.vector.tensor_copy(out=dst, in_=src)
-                else:
-                    nc.scalar.copy(out=dst, in_=src)
-                halves_bf.append(half)
-            w_q.append([quantize("w%d_%d" % (i, g), halves_bf[g][:], 256) for g in range(2)])
+        w_q = []
+        for i in range(3):
+            grouped = keep.tile([P, PACK * H], BF16, name="w_bf%d" % i, tag="w_bf%d" % i, align_bytes=64)
+            dst = grouped[:].rearrange("p (t m j) -> p m j t", t=PACK, j=PACK)
+            for raw, (m0, m1, share) in zip(w_raw[i], W_LOADS[i]):
+                shared_copy(dst[:, m0:m1], raw[:].rearrange("p j (m t) -> p m j t", t=PACK), share)
+            width = H // W_QUANT[i]
+            w_q.append([quantize("w%d_%d" % (i, g), grouped[:, PACK * width * g : PACK * width * (g + 1)], width) for g in range(W_QUANT[i])])
+            if i == 0:
+                x_q.append(quantize("x1", picked[1][:], V, tag="w_bf0"))
 
         def w_tile(i, t):
             per = PACK // len(w_q[i])
@@ -123,44 +111,36 @@ def tile_picked_edgeup_silu_e_kernel(tc, xT, eT, w1, w2, w3, w4_words, w4_scales
             return codes[:, cols].bitcast(FP8X4), scales[:, cols]
 
         acc = [psum.tile([P, PACK, BLOCK], F32, name="acc%d" % b) for b in range(BLOCKS)]
-        def x_passes(i, b, ts):
-            for t in ts:
-                cols = slice(b * BLOCK, (b + 1) * BLOCK)
+
+        def node_passes(i, b):
+            cols = slice(b * BLOCK, (b + 1) * BLOCK)
+            for t in range(PACK):
                 wc, ws = w_tile(i, t)
                 nc.tensor.matmul_mx(out=acc[b][:, t, :], lhsT=wc, lhsT_scale=ws,
                                     rhs=x_q[i][0][:, cols].bitcast(FP8X4), rhs_scale=x_q[i][1][:, cols],
                                     start=(i == 0 and t == 0), stop=False)
 
-        for g in range(2):
-            for b in range(BLOCKS):
-                x_passes(0, b, (2 * g, 2 * g + 1))
-
-        e_q = []
-        e_bf = []
         for b in range(BLOCKS):
+            node_passes(0, b)
+
+        h_bf = []
+        for b in range(BLOCKS):
+            node_passes(1, b)
             grouped = keep.tile([P, BLOCK * PACK], BF16, name="e_bf%d" % b, align_bytes=64)
             dst = grouped[:].rearrange("p (c i j) -> p c j i", i=4, j=PACK)
-            src = e_raw[b // 2][:, :, (b % 2) * BLOCK : (b % 2 + 1) * BLOCK].rearrange("p j (c i) -> p c j i", i=4)
-            if b < 2:
-                nc.scalar.copy(out=dst, in_=src)
-            else:
-                nc.vector.tensor_copy(out=dst, in_=src)
-            e_bf.append(grouped)
-        for b in range(BLOCKS):
-            ec, es = quantize("e%d" % b, e_bf[b][:], BLOCK)
-            e_q.append((ec[:], es[:]))
+            shared_copy(dst, e_raw[b].rearrange("p j (c i) -> p c j i", i=4), (BLOCK - E_ON_SCALAR[b]) // 4)
+            ec, es = quantize("e%d" % b, grouped[:], BLOCK)
+            for t in range(PACK):
+                wc, ws = w_tile(2, t)
+                nc.tensor.matmul_mx(out=acc[b][:, t, :], lhsT=wc, lhsT_scale=ws, rhs=ec[:].bitcast(FP8X4), rhs_scale=es[:],
+                                    start=False, stop=(t == PACK - 1))
+            hidden = keep.tile([P, BLOCK * PACK], BF16, name="h_bf%d" % b, align_bytes=64)
+            nc.scalar.activation(hidden[:].rearrange("p (v t) -> p v t", t=PACK), acc[b][:].rearrange("p t v -> p v t"), SILU, bias=bias[:])
+            h_bf.append(hidden)
 
         out_rows = out.rearrange("(g p) v -> p g v", p=P)
         for b in range(BLOCKS):
-            x_passes(1, b, range(PACK))
-            for t in range(PACK):
-                wc, ws = w_tile(2, t)
-                nc.tensor.matmul_mx(out=acc[b][:, t, :], lhsT=wc, lhsT_scale=ws,
-                                    rhs=e_q[b][0].bitcast(FP8X4), rhs_scale=e_q[b][1],
-                                    start=False, stop=(t == PACK - 1))
-            h_bf = keep.tile([P, BLOCK * PACK], BF16, name="h_bf%d" % b, align_bytes=64)
-            nc.scalar.activation(h_bf[:].rearrange("p (v t) -> p v t", t=PACK), acc[b][:].rearrange("p t v -> p v t"), SILU, bias=bias[:])
-            hc, hs = quantize("h%d" % b, h_bf[:], BLOCK)
+            hc, hs = quantize("h%d" % b, h_bf[b][:], BLOCK)
             last = b == BLOCKS - 1
             res = psum.tile([P, 2, BLOCK], F32, name="res%d" % b)
             halves = [res[:, 0, :], res[:, 1, :]]

@@ -19,10 +19,9 @@ P = 128
 PACK = 4
 BLOCK = 128
 BLOCKS = V // BLOCK
-X_LOADS = ((0, 0, 1024, 0), (0, 1024, 2048, 672), (1, 0, 1024, 0), (1, 1024, 1536, 512), (1, 1536, 1792, 256), (1, 1792, 2048, 176))
-W_LOADS = (((0, 64, 0), (64, 128, 0)), ((0, 64, 0), (64, 128, 0)), ((0, 64, 32), (64, 128, 44)))
-W_QUANT = (1, 1, 2)
-E_LOADS = ((0, 1), (1, 2), (2, 3), (3, 4))
+X_LOADS = ((0, 0, 1024, 0), (0, 1024, 2048, 672), (1, 0, 1024, 0), (1, 1024, 1536, 512), (1, 1536, 2048, 336))
+W_LOADS = (((0, 128, (0, 0)),), ((0, 128, (128, 0)),), ((0, 128, (128, 40)),))
+E_LOADS = ((0, 2), (2, 3), (3, 4))
 E_ON_SCALAR = (128, 128, 0, 0)
 
 
@@ -95,14 +94,19 @@ def tile_picked_edgeup_silu_e_kernel(tc, xT, eT, w1, w2, w3, w4_words, w4_scales
 
         w_q = []
         for i in range(3):
-            grouped = keep.tile([P, PACK * H], BF16, name="w_bf%d" % i, tag="w_bf%d" % i, align_bytes=64)
-            dst = grouped[:].rearrange("p (t m j) -> p m j t", t=PACK, j=PACK)
-            for raw, (m0, m1, share) in zip(w_raw[i], W_LOADS[i]):
-                shared_copy(dst[:, m0:m1], raw[:].rearrange("p j (m t) -> p m j t", t=PACK), share)
-            width = H // W_QUANT[i]
-            w_q.append([quantize("w%d_%d" % (i, g), grouped[:, PACK * width * g : PACK * width * (g + 1)], width) for g in range(W_QUANT[i])])
-            if i == 0:
-                x_q.append(quantize("x1", picked[1][:], V, tag="w_bf0"))
+            halves = []
+            for g in range(2):
+                half = keep.tile([P, 2 * H], BF16, name="w_bf%d_%d" % (i, g), tag="w_bf%d_%d" % (i, g), align_bytes=64)
+                dst = half[:].rearrange("p (t m j) -> p m j t", t=2, j=PACK)
+                for raw, (m0, m1, shares) in zip(w_raw[i], W_LOADS[i]):
+                    src = raw[:].rearrange("p j (m t) -> p m j t", t=PACK)[:, :, :, 2 * g : 2 * g + 2]
+                    shared_copy(dst[:, m0:m1], src, shares[g])
+                halves.append(half)
+            w_q.append([])
+            for g in range(2):
+                w_q[i].append(quantize("w%d_%d" % (i, g), halves[g][:], H // 2))
+                if i == 0 and g == 0:
+                    x_q.append(quantize("x1", picked[1][:], V, tag="w_bf0_0"))
 
         def w_tile(i, t):
             per = PACK // len(w_q[i])

@@ -19,8 +19,9 @@ P = 128
 PACK = 4
 BLOCK = 128
 BLOCKS = V // BLOCK
-X_LOADS = ((0, 0, 1024, 0), (0, 1024, 2048, 672), (1, 0, 1024, 0), (1, 1024, 1536, 512), (1, 1536, 2048, 336))
+X_LOADS = ((0, 0, 1024, 688), (0, 1024, 2048, 688), (1, 0, 1024, 320), (1, 1024, 1536, 512), (1, 1536, 2048, 344))
 W_LOADS = (((0, 128, (0, 0)),), ((0, 128, (128, 0)),), ((0, 128, (128, 40)),))
+PIECES = ((0, 256, True), (256, 512, True), (512, 1024, False))
 E_LOADS = ((0, 2), (2, 3), (3, 4))
 E_ON_SCALAR = (128, 128, 0, 0)
 
@@ -81,16 +82,24 @@ def tile_picked_edgeup_silu_e_kernel(tc, xT, eT, w1, w2, w3, w4_words, w4_scales
             nc.gpsimd.dma_start(out=w4_s[32 * q : 32 * q + 4, :].bitcast(I32), in_=w4_scales[0, 4 * q : 4 * q + 4, :].bitcast(I32))
 
         pairs = [keep.tile([P, T], U32, name="pairs%d" % u, align_bytes=64) for u in range(2)]
-        picked = [keep.tile([P, V * PACK], BF16, name="picked%d" % s, align_bytes=64) for s in range(2)]
+        found = [keep.tile([P, 2, v1 - v0], U32, name="found%d" % v0, tag="found%d" % v0, align_bytes=64) for v0, v1, on_scalar in PIECES]
         for u in range(2):
             for i, (uu, c0, c1, share) in enumerate(X_LOADS):
                 if uu == u:
                     dst = pairs[u][:].bitcast(BF16).rearrange("p (c i e) -> p c e i", i=4, e=2)
                     shared_copy(dst[:, c0 // 4 : c1 // 4], x_raw[i][:].rearrange("p e (c i) -> p c e i", i=4), share // 4)
-            for s in range(2):
-                dst = picked[s][:].bitcast(U32).rearrange("p (v u) -> p v u", u=2)[:, :, u]
-                nc.vector.tensor_copy(out=dst, in_=pairs[u][:].indirect(offsets[:, 32 * s : 32 * (s + 1)]))
-        x_q = [quantize("x0", picked[0][:], V)]
+            for words, (v0, v1, on_scalar) in zip(found, PIECES):
+                nc.vector.tensor_copy(out=words[:, u, :], in_=pairs[u][:].indirect(offsets[:, v0 // 16 : v1 // 16]))
+
+        def weave(dst, words, word):
+            return dict(out=dst.bitcast(word).rearrange("p (v u) -> p v u", u=2), in_=words[:].bitcast(word).rearrange("p u v -> p v u"))
+
+        sources = keep.tile([P, V * PACK], BF16, name="sources", align_bytes=64)
+        for words, (v0, v1, on_scalar) in zip(found[:-1], PIECES):
+            nc.scalar.copy(**weave(sources[:, PACK * v0 : PACK * v1], words, U32))
+        x_q = [quantize("x0", sources[:], V)]
+        targets = keep.tile([P, V * PACK], BF16, name="targets", tag="found256", align_bytes=64)
+        nc.vector.tensor_copy(**weave(targets[:], found[-1], I32))
 
         w_q = []
         for i in range(3):
@@ -106,7 +115,7 @@ def tile_picked_edgeup_silu_e_kernel(tc, xT, eT, w1, w2, w3, w4_words, w4_scales
             for g in range(2):
                 w_q[i].append(quantize("w%d_%d" % (i, g), halves[g][:], H // 2))
                 if i == 0 and g == 0:
-                    x_q.append(quantize("x1", picked[1][:], V, tag="w_bf0_0"))
+                    x_q.append(quantize("x1", targets[:], V, tag="w_bf0_0"))
 
         def w_tile(i, t):
             per = PACK // len(w_q[i])

@@ -19,10 +19,11 @@ P = 128
 PACK = 4
 BLOCK = 128
 BLOCKS = V // BLOCK
-X_LOADS = ((0, 0, 1024, 688), (0, 1024, 2048, 688), (1, 0, 1024, 320), (1, 1024, 1536, 512), (1, 1536, 2048, 344))
-W_LOADS = (((0, 128, (0, 0)),), ((0, 128, (128, 0)),), ((0, 128, (128, 40)),))
+X_LOADS = ((0, 0, 1024, 688), (0, 1024, 2048, 688), (1, 0, 1024, 320), (1, 1024, 1536, 512), (1, 1536, 1792, 0), (1, 1792, 2048, 176))
+W_LOADS = (((0, 128, (0, 0)),), ((0, 128, (64, 0)),), ((0, 128, (128, 0)),))
 PIECES = ((0, 256, True), (256, 512, True), (512, 1024, False))
-E_LOADS = ((0, 2), (2, 3), (3, 4))
+OUT_STEPS = ((0, 1, "v"), (1, 2, "v"), (2, 3, "s"), (3, 4, "vs"))
+E_LOADS = ((0, 2), (2, 4))
 E_ON_SCALAR = (128, 128, 0, 0)
 
 
@@ -65,7 +66,7 @@ def tile_picked_edgeup_silu_e_kernel(tc, xT, eT, w1, w2, w3, w4_words, w4_scales
             w_rows = w.rearrange("(p j) c -> p j c", j=PACK)
             parts = []
             for m0, m1, share in W_LOADS[i]:
-                raw = keep.tile([P, PACK, PACK * (m1 - m0)], F32, name="w_raw%d_%d" % (i, m0))
+                raw = keep.tile([P, PACK, PACK * (m1 - m0)], F32, name="w_raw%d_%d" % (i, m0), tag="w_raw%d_%d" % (i, m0), align_bytes=64)
                 nc.sync.dma_start(out=raw[:], in_=w_rows[:, :, PACK * m0 : PACK * m1])
                 parts.append(raw)
             w_raw.append(parts)
@@ -103,19 +104,21 @@ def tile_picked_edgeup_silu_e_kernel(tc, xT, eT, w1, w2, w3, w4_words, w4_scales
 
         w_q = []
         for i in range(3):
-            halves = []
-            for g in range(2):
+            halves = {}
+            for g in (0, 1) if i == 0 else (1, 0):
                 half = keep.tile([P, 2 * H], BF16, name="w_bf%d_%d" % (i, g), tag="w_bf%d_%d" % (i, g), align_bytes=64)
                 dst = half[:].rearrange("p (t m j) -> p m j t", t=2, j=PACK)
                 for raw, (m0, m1, shares) in zip(w_raw[i], W_LOADS[i]):
                     src = raw[:].rearrange("p j (m t) -> p m j t", t=PACK)[:, :, :, 2 * g : 2 * g + 2]
                     shared_copy(dst[:, m0:m1], src, shares[g])
-                halves.append(half)
-            w_q.append([])
-            for g in range(2):
-                w_q[i].append(quantize("w%d_%d" % (i, g), halves[g][:], H // 2))
-                if i == 0 and g == 0:
-                    x_q.append(quantize("x1", targets[:], V, tag="w_bf0_0"))
+                halves[g] = half
+            if i == 0:
+                first = quantize("w0_0", halves[0][:], H // 2)
+                x_q.append(quantize("x1", targets[:], V, tag="w_bf0_0"))
+                w_q.append([first, quantize("w0_1", halves[1][:], H // 2)])
+            else:
+                second = quantize("w%d_1" % i, halves[1][:], H // 2)
+                w_q.append([quantize("w%d_0" % i, halves[0][:], H // 2, tag="w_raw%d_0" % i), second])
 
         def w_tile(i, t):
             per = PACK // len(w_q[i])
@@ -123,11 +126,11 @@ def tile_picked_edgeup_silu_e_kernel(tc, xT, eT, w1, w2, w3, w4_words, w4_scales
             cols = slice((t % per) * P, (t % per + 1) * P)
             return codes[:, cols].bitcast(FP8X4), scales[:, cols]
 
-        acc = [psum.tile([P, PACK, BLOCK], F32, name="acc%d" % b) for b in range(BLOCKS)]
+        acc = [psum.tile([P, PACK, BLOCK], F32, name="acc%d" % b, tag="acc%d" % b) for b in range(BLOCKS)]
 
         def node_passes(i, b):
             cols = slice(b * BLOCK, (b + 1) * BLOCK)
-            for t in range(PACK):
+            for t in (0, 1, 2, 3) if i == 0 else (2, 3, 0, 1):
                 wc, ws = w_tile(i, t)
                 nc.tensor.matmul_mx(out=acc[b][:, t, :], lhsT=wc, lhsT_scale=ws,
                                     rhs=x_q[i][0][:, cols].bitcast(FP8X4), rhs_scale=x_q[i][1][:, cols],
@@ -136,38 +139,39 @@ def tile_picked_edgeup_silu_e_kernel(tc, xT, eT, w1, w2, w3, w4_words, w4_scales
         for b in range(BLOCKS):
             node_passes(0, b)
 
-        h_bf = []
+        h_bf = keep.tile([P, V * PACK], BF16, name="h_bf", align_bytes=64)
         for b in range(BLOCKS):
             node_passes(1, b)
             grouped = keep.tile([P, BLOCK * PACK], BF16, name="e_bf%d" % b, align_bytes=64)
             dst = grouped[:].rearrange("p (c i j) -> p c j i", i=4, j=PACK)
             shared_copy(dst, e_raw[b].rearrange("p j (c i) -> p c j i", i=4), (BLOCK - E_ON_SCALAR[b]) // 4)
             ec, es = quantize("e%d" % b, grouped[:], BLOCK)
-            for t in range(PACK):
+            for t in (2, 3, 0, 1):
                 wc, ws = w_tile(2, t)
                 nc.tensor.matmul_mx(out=acc[b][:, t, :], lhsT=wc, lhsT_scale=ws, rhs=ec[:].bitcast(FP8X4), rhs_scale=es[:],
-                                    start=False, stop=(t == PACK - 1))
-            hidden = keep.tile([P, BLOCK * PACK], BF16, name="h_bf%d" % b, align_bytes=64)
-            nc.scalar.activation(hidden[:].rearrange("p (v t) -> p v t", t=PACK), acc[b][:].rearrange("p t v -> p v t"), SILU, bias=bias[:])
-            h_bf.append(hidden)
+                                    start=False, stop=(t == 1))
+            hidden = h_bf[:, PACK * BLOCK * b : PACK * BLOCK * (b + 1)]
+            nc.scalar.activation(hidden.rearrange("p (v t) -> p v t", t=PACK), acc[b][:].rearrange("p t v -> p v t"), SILU, bias=bias[:])
 
         out_rows = out.rearrange("(g p) v -> p g v", p=P)
-        for b in range(BLOCKS):
-            hc, hs = quantize("h%d" % b, h_bf[b][:], BLOCK)
-            last = b == BLOCKS - 1
-            res = psum.tile([P, 2, BLOCK], F32, name="res%d" % b)
+        for b0, b1, engines in OUT_STEPS:
+            width = BLOCK * (b1 - b0)
+            hc, hs = quantize("h%d" % b0, h_bf[:, PACK * BLOCK * b0 : PACK * BLOCK * b1], width)
+            res = psum.tile([P, 2, width], F32, name="res%d" % b0)
             halves = [res[:, 0, :], res[:, 1, :]]
-            if last:
-                other = psum.tile([P, BLOCK], F32, name="res_other", tag="acc0")
+            if len(engines) == 2:
+                other = psum.tile([P, width], F32, name="res_other%d" % b0, tag="acc0")
                 halves[1] = other[:]
             for g in range(2):
                 nc.tensor.matmul_mx(out=halves[g], lhsT=w4_w[:, 2 * P * g : 2 * P * (g + 1)].bitcast(FP4X4),
                                     lhsT_scale=w4_s[:, P * g : P * (g + 1)],
                                     rhs=hc[:].bitcast(FP8X4), rhs_scale=hs[:], start=True, stop=True)
-            res_sb = keep.tile([P, 2, BLOCK], F32, name="res_sb%d" % b)
-            if last:
+            res_sb = keep.tile([P, 2, width], F32, name="res_sb%d" % b0)
+            if engines == "vs":
                 nc.vector.tensor_copy(out=res_sb[:, 0, :], in_=halves[0])
                 nc.scalar.copy(out=res_sb[:, 1, :], in_=halves[1])
-            else:
+            elif engines == "v":
                 nc.vector.tensor_copy(out=res_sb[:], in_=res[:])
-            nc.sync.dma_start(out=out_rows[:, :, b * BLOCK : (b + 1) * BLOCK], in_=res_sb[:])
+            else:
+                nc.scalar.copy(out=res_sb[:], in_=res[:])
+            nc.sync.dma_start(out=out_rows[:, :, BLOCK * b0 : BLOCK * b1], in_=res_sb[:])

@@ -20,10 +20,10 @@ PACK = 4
 BLOCK = 128
 BLOCKS = V // BLOCK
 X_LOADS = ((0, 0, 1024, 688), (0, 1024, 2048, 688), (1, 0, 1024, 320), (1, 1024, 1536, 512), (1, 1536, 1792, 0), (1, 1792, 2048, 176))
-W_LOADS = (((0, 128, (0, 0)),), ((0, 128, (64, 0)),), ((0, 128, (128, 0)),))
+W_LOADS = (((0, 128, (0, 0)),), ((0, 128, (128, 0)),), ((0, 64, (0, 0)), (64, 128, (64, 64))))
 PIECES = ((0, 256, True), (256, 512, True), (512, 1024, False))
 OUT_STEPS = ((0, 1, "v"), (1, 2, "v"), (2, 3, "s"), (3, 4, "vs"))
-E_LOADS = ((0, 2), (2, 4))
+E_LOADS = ((0, 1), (1, 2), (2, 3), (3, 4))
 E_ON_SCALAR = (128, 128, 0, 0)
 
 
@@ -73,7 +73,7 @@ def tile_picked_edgeup_silu_e_kernel(tc, xT, eT, w1, w2, w3, w4_words, w4_scales
         e_rows = eT.rearrange("(p j) v -> p j v", j=PACK)
         e_raw = []
         for b0, b1 in E_LOADS:
-            raw = keep.tile([P, PACK, BLOCK * (b1 - b0)], F32, name="e_raw%d" % b0)
+            raw = keep.tile([P, PACK, BLOCK * (b1 - b0)], F32, name="e_raw%d" % b0, tag="e_raw%d" % b0, align_bytes=64)
             nc.sync.dma_start(out=raw[:], in_=e_rows[:, :, BLOCK * b0 : BLOCK * b1])
             for b in range(b0, b1):
                 e_raw.append(raw[:, :, BLOCK * (b - b0) : BLOCK * (b - b0 + 1)])
@@ -102,10 +102,16 @@ def tile_picked_edgeup_silu_e_kernel(tc, xT, eT, w1, w2, w3, w4_words, w4_scales
         targets = keep.tile([P, V * PACK], BF16, name="targets", tag="found256", align_bytes=64)
         nc.vector.tensor_copy(**weave(targets[:], found[-1], I32))
 
+        def edge_codes(b):
+            grouped = keep.tile([P, BLOCK * PACK], BF16, name="e_bf%d" % b, align_bytes=64)
+            dst = grouped[:].rearrange("p (c i j) -> p c j i", i=4, j=PACK)
+            shared_copy(dst, e_raw[b].rearrange("p j (c i) -> p c j i", i=4), (BLOCK - E_ON_SCALAR[b]) // 4)
+            return quantize("e%d" % b, grouped[:], BLOCK)
+
         w_q = []
         for i in range(3):
             halves = {}
-            for g in (0, 1) if i == 0 else (1, 0):
+            for g in (1, 0) if i == 1 else (0, 1):
                 half = keep.tile([P, 2 * H], BF16, name="w_bf%d_%d" % (i, g), tag="w_bf%d_%d" % (i, g), align_bytes=64)
                 dst = half[:].rearrange("p (t m j) -> p m j t", t=2, j=PACK)
                 for raw, (m0, m1, shares) in zip(w_raw[i], W_LOADS[i]):
@@ -116,6 +122,10 @@ def tile_picked_edgeup_silu_e_kernel(tc, xT, eT, w1, w2, w3, w4_words, w4_scales
                 first = quantize("w0_0", halves[0][:], H // 2)
                 x_q.append(quantize("x1", targets[:], V, tag="w_bf0_0"))
                 w_q.append([first, quantize("w0_1", halves[1][:], H // 2)])
+            elif i == 2:
+                first = quantize("w2_0", halves[0][:], H // 2)
+                e_first = edge_codes(0)
+                w_q.append([first, quantize("w2_1", halves[1][:], H // 2, tag="e_raw0")])
             else:
                 second = quantize("w%d_1" % i, halves[1][:], H // 2)
                 w_q.append([quantize("w%d_0" % i, halves[0][:], H // 2, tag="w_raw%d_0" % i), second])
@@ -142,14 +152,11 @@ def tile_picked_edgeup_silu_e_kernel(tc, xT, eT, w1, w2, w3, w4_words, w4_scales
         h_bf = keep.tile([P, V * PACK], BF16, name="h_bf", align_bytes=64)
         for b in range(BLOCKS):
             node_passes(1, b)
-            grouped = keep.tile([P, BLOCK * PACK], BF16, name="e_bf%d" % b, align_bytes=64)
-            dst = grouped[:].rearrange("p (c i j) -> p c j i", i=4, j=PACK)
-            shared_copy(dst, e_raw[b].rearrange("p j (c i) -> p c j i", i=4), (BLOCK - E_ON_SCALAR[b]) // 4)
-            ec, es = quantize("e%d" % b, grouped[:], BLOCK)
-            for t in (2, 3, 0, 1):
+            ec, es = e_first if b == 0 else edge_codes(b)
+            for t in range(PACK):
                 wc, ws = w_tile(2, t)
                 nc.tensor.matmul_mx(out=acc[b][:, t, :], lhsT=wc, lhsT_scale=ws, rhs=ec[:].bitcast(FP8X4), rhs_scale=es[:],
-                                    start=False, stop=(t == 1))
+                                    start=False, stop=(t == PACK - 1))
             hidden = h_bf[:, PACK * BLOCK * b : PACK * BLOCK * (b + 1)]
             nc.scalar.activation(hidden.rearrange("p (v t) -> p v t", t=PACK), acc[b][:].rearrange("p t v -> p v t"), SILU, bias=bias[:])
 

@@ -19,7 +19,8 @@ P = 128
 PACK = 4
 BLOCK = 128
 BLOCKS = V // BLOCK
-X_LOADS = ((0, 0, 1024, 688), (0, 1024, 2048, 688), (1, 0, 1024, 320), (1, 1024, 1536, 512), (1, 1536, 1792, 0), (1, 1792, 2048, 176))
+X_LOADS = ((0, 3072), (3072, 4096), (4096, 6656), (6656, 7424), (7424, 7936), (7936, 8192))
+X_CASTS = ((0, 0, 1024, 688), (0, 1024, 2048, 688), (1, 0, 512, 0), (1, 512, 1280, 640), (1, 1280, 1792, 320), (1, 1792, 2048, 176))
 W_LOADS = (((0, 128, (0, 0)),), ((0, 128, (128, 0)),), ((0, 64, (0, 0)), (64, 128, (64, 64))))
 PIECES = ((0, 256, True), (256, 512, True), (512, 1024, False))
 OUT_STEPS = ((0, 1, "v"), (1, 2, "v"), (2, 3, "s"), (3, 4, "vs"))
@@ -52,13 +53,11 @@ def tile_picked_edgeup_silu_e_kernel(tc, xT, eT, w1, w2, w3, w4_words, w4_scales
         w4_s = keep.tile([P, N], U8, name="w4_s", align_bytes=64)
         nc.vector.memset(w4_s[:].bitcast(I32), 0)
 
-        x_rows = xT.rearrange("(p j) t -> p j t", j=PACK)
-        x_raw = []
+        x_runs = xT.rearrange("(p j) t -> p (j t)", j=PACK)
+        x_raw = keep.tile([P, PACK * T], F32, name="x_raw")
         offsets = keep.tile([P, S // 16], U16, name="offsets")
-        for i, (u, c0, c1, share) in enumerate(X_LOADS):
-            raw = keep.tile([P, 2, c1 - c0], F32, name="x_raw%d" % i)
-            nc.sync.dma_start(out=raw[:], in_=x_rows[:, 2 * u : 2 * u + 2, c0:c1])
-            x_raw.append(raw)
+        for i, (a0, a1) in enumerate(X_LOADS):
+            nc.sync.dma_start(out=x_raw[:, a0:a1], in_=x_runs[:, a0:a1])
             if i == 0:
                 nc.sync.dma_start(offsets[:], offs)
         w_raw = []
@@ -85,10 +84,11 @@ def tile_picked_edgeup_silu_e_kernel(tc, xT, eT, w1, w2, w3, w4_words, w4_scales
         pairs = [keep.tile([P, T], U32, name="pairs%d" % u, align_bytes=64) for u in range(2)]
         found = [keep.tile([P, 2, v1 - v0], U32, name="found%d" % v0, tag="found%d" % v0, align_bytes=64) for v0, v1, on_scalar in PIECES]
         for u in range(2):
-            for i, (uu, c0, c1, share) in enumerate(X_LOADS):
+            for i, (uu, c0, c1, share) in enumerate(X_CASTS):
                 if uu == u:
                     dst = pairs[u][:].bitcast(BF16).rearrange("p (c i e) -> p c e i", i=4, e=2)
-                    shared_copy(dst[:, c0 // 4 : c1 // 4], x_raw[i][:].rearrange("p e (c i) -> p c e i", i=4), share // 4)
+                    rows = x_raw[:, 2 * T * u : 2 * T * (u + 1)].rearrange("p (e c i) -> p c e i", e=2, i=4)
+                    shared_copy(dst[:, c0 // 4 : c1 // 4], rows[:, c0 // 4 : c1 // 4], share // 4)
             for words, (v0, v1, on_scalar) in zip(found, PIECES):
                 nc.vector.tensor_copy(out=words[:, u, :], in_=pairs[u][:].indirect(offsets[:, v0 // 16 : v1 // 16]))
 

@@ -69,6 +69,9 @@ def tile_picked_edgeup_silu_e_kernel(tc, xT, eT, w1, w2, w3, w4_words, w4_scales
                 nc.sync.dma_start(out=raw[:], in_=w_rows[:, :, PACK * m0 : PACK * m1])
                 parts.append(raw)
             w_raw.append(parts)
+            if i == 0:
+                for q in range(4):
+                    nc.sync.dma_start(out=w4_s[32 * q : 32 * q + 4, :].bitcast(I32), in_=w4_scales[0, 4 * q : 4 * q + 4, :].bitcast(I32))
         e_rows = eT.rearrange("(p j) v -> p j v", j=PACK)
         e_raw = []
         for b0, b1 in E_LOADS:
@@ -78,8 +81,6 @@ def tile_picked_edgeup_silu_e_kernel(tc, xT, eT, w1, w2, w3, w4_words, w4_scales
                 e_raw.append(raw[:, :, BLOCK * (b - b0) : BLOCK * (b - b0 + 1)])
         w4_w = keep.tile([P, 2 * N], U8, name="w4_w", align_bytes=64)
         nc.sync.dma_start(out=w4_w[:], in_=w4_words[0])
-        for q in range(4):
-            nc.gpsimd.dma_start(out=w4_s[32 * q : 32 * q + 4, :].bitcast(I32), in_=w4_scales[0, 4 * q : 4 * q + 4, :].bitcast(I32))
 
         pairs = [keep.tile([P, T], U32, name="pairs%d" % u, align_bytes=64) for u in range(2)]
         found = [keep.tile([P, 2, v1 - v0], U32, name="found%d" % v0, tag="found%d" % v0, align_bytes=64) for v0, v1, on_scalar in PIECES]

@@ -20,9 +20,10 @@ PACK = 4
 BLOCK = 128
 BLOCKS = V // BLOCK
 X_LOADS = ((0, 3072), (3072, 4096), (4096, 6656), (6656, 7424), (7424, 7936), (7936, 8192))
-X_CASTS = ((0, 0, 1024, 688), (0, 1024, 2048, 688), (1, 0, 512, 0), (1, 512, 1280, 640), (1, 1280, 1792, 320), (1, 1792, 2048, 176))
+X_CASTS = ((0, 0, 1024, 688), (0, 1024, 2048, 688), (1, 0, 512, 0), (1, 512, 1280, 576), (1, 1280, 1792, 320), (1, 1792, 2048, 160))
 W_LOADS = (((0, 128, (0, 0)),), ((0, 128, (128, 0)),), ((0, 64, (0, 0)), (64, 128, (64, 64))))
-PIECES = ((0, 256, True), (256, 512, True), (512, 1024, False))
+W_RUNS = (((0, 2048),), ((0, 2048),), ((0, 1792), (1792, 2048)))
+GATHERS = (((0, 512), (512, 1024)), ((0, 256), (256, 512), (512, 1024)))
 OUT_STEPS = ((0, 1, "v"), (1, 2, "v"), (2, 3, "s"), (3, 4, "vs"))
 E_LOADS = ((0, 1), (1, 2), (2, 3), (3, 4))
 E_ON_SCALAR = (128, 128, 0, 0)
@@ -62,13 +63,11 @@ def tile_picked_edgeup_silu_e_kernel(tc, xT, eT, w1, w2, w3, w4_words, w4_scales
                 nc.sync.dma_start(offsets[:], offs)
         w_raw = []
         for i, w in enumerate((w1, w2, w3)):
-            w_rows = w.rearrange("(p j) c -> p j c", j=PACK)
-            parts = []
-            for m0, m1, share in W_LOADS[i]:
-                raw = keep.tile([P, PACK, PACK * (m1 - m0)], F32, name="w_raw%d_%d" % (i, m0), tag="w_raw%d_%d" % (i, m0), align_bytes=64)
-                nc.sync.dma_start(out=raw[:], in_=w_rows[:, :, PACK * m0 : PACK * m1])
-                parts.append(raw)
-            w_raw.append(parts)
+            w_runs = w.rearrange("(p j) c -> p (j c)", j=PACK)
+            raw = keep.tile([P, PACK * H], F32, name="w_raw%d" % i, tag="w_raw%d" % i, align_bytes=64)
+            for a0, a1 in W_RUNS[i]:
+                nc.sync.dma_start(out=raw[:, a0:a1], in_=w_runs[:, a0:a1])
+            w_raw.append(raw)
             if i == 0:
                 for q in range(4):
                     nc.sync.dma_start(out=w4_s[32 * q : 32 * q + 4, :].bitcast(I32), in_=w4_scales[0, 4 * q : 4 * q + 4, :].bitcast(I32))
@@ -83,25 +82,26 @@ def tile_picked_edgeup_silu_e_kernel(tc, xT, eT, w1, w2, w3, w4_words, w4_scales
         nc.sync.dma_start(out=w4_w[:], in_=w4_words[0])
 
         pairs = [keep.tile([P, T], U32, name="pairs%d" % u, align_bytes=64) for u in range(2)]
-        found = [keep.tile([P, 2, v1 - v0], U32, name="found%d" % v0, tag="found%d" % v0, align_bytes=64) for v0, v1, on_scalar in PIECES]
+        found = [keep.tile([P, 2, V], U32, name="found%d" % side, tag="found%d" % side, align_bytes=64) for side in range(2)]
         for u in range(2):
             for i, (uu, c0, c1, share) in enumerate(X_CASTS):
                 if uu == u:
                     dst = pairs[u][:].bitcast(BF16).rearrange("p (c i e) -> p c e i", i=4, e=2)
                     rows = x_raw[:, 2 * T * u : 2 * T * (u + 1)].rearrange("p (e c i) -> p c e i", e=2, i=4)
                     shared_copy(dst[:, c0 // 4 : c1 // 4], rows[:, c0 // 4 : c1 // 4], share // 4)
-            for words, (v0, v1, on_scalar) in zip(found, PIECES):
-                nc.vector.tensor_copy(out=words[:, u, :], in_=pairs[u][:].indirect(offsets[:, v0 // 16 : v1 // 16]))
+            for v0, v1 in GATHERS[u]:
+                side = v0 // V
+                nc.vector.tensor_copy(out=found[side][:, u, v0 - V * side : v1 - V * side], in_=pairs[u][:].indirect(offsets[:, v0 // 16 : v1 // 16]))
 
         def weave(dst, words, word):
-            return dict(out=dst.bitcast(word).rearrange("p (v u) -> p v u", u=2), in_=words[:].bitcast(word).rearrange("p u v -> p v u"))
+            return dict(out=dst.bitcast(word).rearrange("p (v u) -> p v u", u=2), in_=words.bitcast(word).rearrange("p u v -> p v u"))
 
         sources = keep.tile([P, V * PACK], BF16, name="sources", align_bytes=64)
-        for words, (v0, v1, on_scalar) in zip(found[:-1], PIECES):
-            nc.scalar.copy(**weave(sources[:, PACK * v0 : PACK * v1], words, U32))
+        for v0, v1 in GATHERS[1][:2]:
+            nc.scalar.copy(**weave(sources[:, PACK * v0 : PACK * v1], found[0][:, :, v0:v1], U32))
         x_q = [quantize("x0", sources[:], V)]
-        targets = keep.tile([P, V * PACK], BF16, name="targets", tag="found256", align_bytes=64)
-        nc.vector.tensor_copy(**weave(targets[:], found[-1], I32))
+        targets = keep.tile([P, V * PACK], BF16, name="targets", tag="found0", align_bytes=64)
+        nc.vector.tensor_copy(**weave(targets[:], found[1][:], I32))
 
         def edge_codes(b):
             grouped = keep.tile([P, BLOCK * PACK], BF16, name="e_bf%d" % b, align_bytes=64)
@@ -115,9 +115,9 @@ def tile_picked_edgeup_silu_e_kernel(tc, xT, eT, w1, w2, w3, w4_words, w4_scales
             for g in (1, 0) if i == 1 else (0, 1):
                 half = keep.tile([P, 2 * H], BF16, name="w_bf%d_%d" % (i, g), tag="w_bf%d_%d" % (i, g), align_bytes=64)
                 dst = half[:].rearrange("p (t m j) -> p m j t", t=2, j=PACK)
-                for raw, (m0, m1, shares) in zip(w_raw[i], W_LOADS[i]):
-                    src = raw[:].rearrange("p j (m t) -> p m j t", t=PACK)[:, :, :, 2 * g : 2 * g + 2]
-                    shared_copy(dst[:, m0:m1], src, shares[g])
+                src = w_raw[i][:].rearrange("p (j m t) -> p m j t", j=PACK, t=PACK)[:, :, :, 2 * g : 2 * g + 2]
+                for m0, m1, shares in W_LOADS[i]:
+                    shared_copy(dst[:, m0:m1], src[:, m0:m1], shares[g])
                 halves[g] = half
             if i == 0:
                 first = quantize("w0_0", halves[0][:], H // 2)
@@ -129,7 +129,7 @@ def tile_picked_edgeup_silu_e_kernel(tc, xT, eT, w1, w2, w3, w4_words, w4_scales
                 w_q.append([first, quantize("w2_1", halves[1][:], H // 2, tag="e_raw0")])
             else:
                 second = quantize("w%d_1" % i, halves[1][:], H // 2)
-                w_q.append([quantize("w%d_0" % i, halves[0][:], H // 2, tag="w_raw%d_0" % i), second])
+                w_q.append([quantize("w%d_0" % i, halves[0][:], H // 2, tag="w_raw%d" % i), second])
 
         def w_tile(i, t):
             per = PACK // len(w_q[i])

@@ -19,11 +19,9 @@ P = 128
 PACK = 4
 BLOCK = 128
 BLOCKS = V // BLOCK
-X_LOADS = ((0, 3072), (3072, 4096), (4096, 6656), (6656, 7424), (7424, 7936), (7936, 8192))
-X_CASTS = ((0, 0, 1024, 688), (0, 1024, 2048, 688), (1, 0, 512, 0), (1, 512, 1280, 576), (1, 1280, 1792, 320), (1, 1792, 2048, 160))
 W_LOADS = (((0, 128, (0, 0)),), ((0, 128, (128, 0)),), ((0, 64, (0, 0)), (64, 128, (64, 64))))
 W_RUNS = (((0, 2048),), ((0, 2048),), ((0, 1792), (1792, 2048)))
-GATHERS = (((0, 512), (512, 1024)), ((0, 256), (256, 512), (512, 1024)))
+GATHERS = (((0, 1024),), ((0, 512), (512, 1024)), ((0, 1024),), ((0, 256), (256, 512), (512, 768), (768, 1024)))
 OUT_STEPS = ((0, 1, "v"), (1, 2, "v"), (2, 3, "s"), (3, 4, "vs"))
 E_LOADS = ((0, 1), (1, 2), (2, 3), (3, 4))
 E_ON_SCALAR = (128, 128, 0, 0)
@@ -54,12 +52,14 @@ def tile_picked_edgeup_silu_e_kernel(tc, xT, eT, w1, w2, w3, w4_words, w4_scales
         w4_s = keep.tile([P, N], U8, name="w4_s", align_bytes=64)
         nc.vector.memset(w4_s[:].bitcast(I32), 0)
 
-        x_runs = xT.rearrange("(p j) t -> p (j t)", j=PACK)
-        x_raw = keep.tile([P, PACK * T], F32, name="x_raw")
+        x_rows = xT.rearrange("(p j) t -> p j t", j=PACK)
         offsets = keep.tile([P, S // 16], U16, name="offsets")
-        for i, (a0, a1) in enumerate(X_LOADS):
-            nc.sync.dma_start(out=x_raw[:, a0:a1], in_=x_runs[:, a0:a1])
-            if i == 0:
+        x_raw = []
+        for j in range(PACK):
+            row = keep.tile([P, T], F32, name="x_raw%d" % j, align_bytes=64)
+            nc.sync.dma_start(out=row[:], in_=x_rows[:, j, :])
+            x_raw.append(row)
+            if j == 0:
                 nc.sync.dma_start(offsets[:], offs)
         w_raw = []
         for i, w in enumerate((w1, w2, w3)):
@@ -81,27 +81,23 @@ def tile_picked_edgeup_silu_e_kernel(tc, xT, eT, w1, w2, w3, w4_words, w4_scales
         w4_w = keep.tile([P, 2 * N], U8, name="w4_w", align_bytes=64)
         nc.sync.dma_start(out=w4_w[:], in_=w4_words[0])
 
-        pairs = [keep.tile([P, T], U32, name="pairs%d" % u, align_bytes=64) for u in range(2)]
-        found = [keep.tile([P, 2, V], U32, name="found%d" % side, tag="found%d" % side, align_bytes=64) for side in range(2)]
-        for u in range(2):
-            for i, (uu, c0, c1, share) in enumerate(X_CASTS):
-                if uu == u:
-                    dst = pairs[u][:].bitcast(BF16).rearrange("p (c i e) -> p c e i", i=4, e=2)
-                    rows = x_raw[:, 2 * T * u : 2 * T * (u + 1)].rearrange("p (e c i) -> p c e i", e=2, i=4)
-                    shared_copy(dst[:, c0 // 4 : c1 // 4], rows[:, c0 // 4 : c1 // 4], share // 4)
-            for v0, v1 in GATHERS[u]:
-                side = v0 // V
-                nc.vector.tensor_copy(out=found[side][:, u, v0 - V * side : v1 - V * side], in_=pairs[u][:].indirect(offsets[:, v0 // 16 : v1 // 16]))
+        planes = [keep.tile([P, 2, S], BF16, name="planes%d" % u, align_bytes=64) for u in range(2)]
+        picked = [keep.tile([P, V * PACK], BF16, name="picked%d" % side, align_bytes=64) for side in range(2)]
 
-        def weave(dst, words, word):
-            return dict(out=dst.bitcast(word).rearrange("p (v u) -> p v u", u=2), in_=words.bitcast(word).rearrange("p u v -> p v u"))
+        def place(u, v0, v1):
+            side = v0 // V
+            dst = picked[side][:].rearrange("p (v u e) -> p v u e", u=2, e=2)[:, v0 - V * side : v1 - V * side, u, :]
+            return dict(out=dst, in_=planes[u][:, :, v0:v1].rearrange("p e v -> p v e"))
 
-        sources = keep.tile([P, V * PACK], BF16, name="sources", align_bytes=64)
-        for v0, v1 in GATHERS[1][:2]:
-            nc.scalar.copy(**weave(sources[:, PACK * v0 : PACK * v1], found[0][:, :, v0:v1], U32))
-        x_q = [quantize("x0", sources[:], V)]
-        targets = keep.tile([P, V * PACK], BF16, name="targets", tag="found0", align_bytes=64)
-        nc.vector.tensor_copy(**weave(targets[:], found[1][:], I32))
+        for j in range(PACK):
+            for v0, v1 in GATHERS[j]:
+                nc.vector.tensor_copy(out=planes[j // 2][:, j % 2, v0:v1], in_=x_raw[j][:].indirect(offsets[:, v0 // 16 : v1 // 16]))
+                if j == 1 or (j == 3 and v0 < V):
+                    nc.scalar.copy(**place(j // 2, v0, v1))
+        x_q = [quantize("x0", picked[0][:], V)]
+        targets = picked[1]
+        for v0, v1 in GATHERS[3][2:]:
+            nc.vector.tensor_copy(**place(1, v0, v1))
 
         def edge_codes(b):
             grouped = keep.tile([P, BLOCK * PACK], BF16, name="e_bf%d" % b, align_bytes=64)

@@ -34,8 +34,8 @@ def tile_picked_edgeup_silu_e_kernel(tc, xT, eT, w1, w2, w3, w4_words, w4_scales
         psum = ctx.enter_context(tc.psum_pool(name="psum", bufs=1))
 
         def quantize(name, values, width, tag=None):
-            codes = keep.tile([P, width], U32, name=name + "_codes", tag=tag or name + "_codes", align_bytes=64)
-            scales = keep.tile([P, width], U8, name=name + "_scales", align_bytes=64)
+            codes = keep.tile([P, width], U32, name=name + "_codes", tag=tag or name + "_codes", align_bytes=256)
+            scales = keep.tile([P, width], U8, name=name + "_scales", align_bytes=256)
             nc.vector.quantize_mx(out=codes[:].bitcast(FP8X4), scales=scales[:], in_=values)
             return codes, scales
 
@@ -49,14 +49,14 @@ def tile_picked_edgeup_silu_e_kernel(tc, xT, eT, w1, w2, w3, w4_words, w4_scales
         nc.vector.memset(zero[:], 0.0)
         bias = keep.tile([P, 1], F32, name="bias")
         nc.scalar.activation(bias[:], zero[:], SILU)
-        w4_s = keep.tile([P, N], U8, name="w4_s", align_bytes=64)
+        w4_s = keep.tile([P, N], U8, name="w4_s", align_bytes=256)
         nc.vector.memset(w4_s[:].bitcast(I32), 0)
 
         x_rows = xT.rearrange("(p j) t -> p j t", j=PACK)
-        offsets = keep.tile([P, S // 16], U16, name="offsets")
+        offsets = keep.tile([P, S // 16], U16, name="offsets", align_bytes=256)
         x_raw = []
         for j in range(PACK):
-            row = keep.tile([P, T], F32, name="x_raw%d" % j, align_bytes=64)
+            row = keep.tile([P, T], F32, name="x_raw%d" % j, align_bytes=256)
             nc.sync.dma_start(out=row[:], in_=x_rows[:, j, :])
             x_raw.append(row)
             if j == 0:
@@ -64,7 +64,7 @@ def tile_picked_edgeup_silu_e_kernel(tc, xT, eT, w1, w2, w3, w4_words, w4_scales
         w_raw = []
         for i, w in enumerate((w1, w2, w3)):
             w_runs = w.rearrange("(p j) c -> p (j c)", j=PACK)
-            raw = keep.tile([P, PACK * H], F32, name="w_raw%d" % i, tag="w_raw%d" % i, align_bytes=64)
+            raw = keep.tile([P, PACK * H], F32, name="w_raw%d" % i, tag="w_raw%d" % i, align_bytes=256)
             for a0, a1 in W_RUNS[i]:
                 nc.sync.dma_start(out=raw[:, a0:a1], in_=w_runs[:, a0:a1])
             w_raw.append(raw)
@@ -74,15 +74,15 @@ def tile_picked_edgeup_silu_e_kernel(tc, xT, eT, w1, w2, w3, w4_words, w4_scales
         e_rows = eT.rearrange("(p j) v -> p j v", j=PACK)
         e_raw = []
         for b0, b1 in E_LOADS:
-            raw = keep.tile([P, PACK, BLOCK * (b1 - b0)], F32, name="e_raw%d" % b0, tag="e_raw%d" % b0, align_bytes=64)
+            raw = keep.tile([P, PACK, BLOCK * (b1 - b0)], F32, name="e_raw%d" % b0, tag="e_raw%d" % b0, align_bytes=256)
             nc.sync.dma_start(out=raw[:], in_=e_rows[:, :, BLOCK * b0 : BLOCK * b1])
             for b in range(b0, b1):
                 e_raw.append(raw[:, :, BLOCK * (b - b0) : BLOCK * (b - b0 + 1)])
-        w4_w = keep.tile([P, 2 * N], U8, name="w4_w", align_bytes=64)
+        w4_w = keep.tile([P, 2 * N], U8, name="w4_w", align_bytes=256)
         nc.sync.dma_start(out=w4_w[:], in_=w4_words[0])
 
-        planes = [keep.tile([P, 2, S], BF16, name="planes%d" % u, align_bytes=64) for u in range(2)]
-        picked = [keep.tile([P, V * PACK], BF16, name="picked%d" % side, align_bytes=64) for side in range(2)]
+        planes = [keep.tile([P, 2, S], BF16, name="planes%d" % u, align_bytes=256) for u in range(2)]
+        picked = [keep.tile([P, V * PACK], BF16, name="picked%d" % side, align_bytes=256) for side in range(2)]
 
         def place(u, v0, v1):
             side = v0 // V
@@ -100,7 +100,7 @@ def tile_picked_edgeup_silu_e_kernel(tc, xT, eT, w1, w2, w3, w4_words, w4_scales
             nc.vector.tensor_copy(**place(1, v0, v1))
 
         def edge_codes(b):
-            grouped = keep.tile([P, BLOCK * PACK], BF16, name="e_bf%d" % b, align_bytes=64)
+            grouped = keep.tile([P, BLOCK * PACK], BF16, name="e_bf%d" % b, align_bytes=256)
             dst = grouped[:].rearrange("p (c i j) -> p c j i", i=4, j=PACK)
             shared_copy(dst, e_raw[b].rearrange("p j (c i) -> p c j i", i=4), (BLOCK - E_ON_SCALAR[b]) // 4)
             return quantize("e%d" % b, grouped[:], BLOCK)
@@ -109,7 +109,7 @@ def tile_picked_edgeup_silu_e_kernel(tc, xT, eT, w1, w2, w3, w4_words, w4_scales
         for i in range(3):
             halves = {}
             for g in (1, 0) if i == 1 else (0, 1):
-                half = keep.tile([P, 2 * H], BF16, name="w_bf%d_%d" % (i, g), tag="w_bf%d_%d" % (i, g), align_bytes=64)
+                half = keep.tile([P, 2 * H], BF16, name="w_bf%d_%d" % (i, g), tag="w_bf%d_%d" % (i, g), align_bytes=256)
                 dst = half[:].rearrange("p (t m j) -> p m j t", t=2, j=PACK)
                 src = w_raw[i][:].rearrange("p (j m t) -> p m j t", j=PACK, t=PACK)[:, :, :, 2 * g : 2 * g + 2]
                 for m0, m1, shares in W_LOADS[i]:
@@ -146,7 +146,7 @@ def tile_picked_edgeup_silu_e_kernel(tc, xT, eT, w1, w2, w3, w4_words, w4_scales
         for b in range(BLOCKS):
             node_passes(0, b)
 
-        h_bf = keep.tile([P, V * PACK], BF16, name="h_bf", align_bytes=64)
+        h_bf = keep.tile([P, V * PACK], BF16, name="h_bf", align_bytes=256)
         for b in range(BLOCKS):
             node_passes(1, b)
             ec, es = e_first if b == 0 else edge_codes(b)
@@ -170,7 +170,7 @@ def tile_picked_edgeup_silu_e_kernel(tc, xT, eT, w1, w2, w3, w4_words, w4_scales
                 nc.tensor.matmul_mx(out=halves[g], lhsT=w4_w[:, 2 * P * g : 2 * P * (g + 1)].bitcast(FP4X4),
                                     lhsT_scale=w4_s[:, P * g : P * (g + 1)],
                                     rhs=hc[:].bitcast(FP8X4), rhs_scale=hs[:], start=True, stop=True)
-            res_sb = keep.tile([P, 2, width], F32, name="res_sb%d" % b0)
+            res_sb = keep.tile([P, 2, width], F32, name="res_sb%d" % b0, align_bytes=256)
             if engines == "vs":
                 nc.vector.tensor_copy(out=res_sb[:, 0, :], in_=halves[0])
                 nc.scalar.copy(out=res_sb[:, 1, :], in_=halves[1])
@@ -178,4 +178,8 @@ def tile_picked_edgeup_silu_e_kernel(tc, xT, eT, w1, w2, w3, w4_words, w4_scales
                 nc.vector.tensor_copy(out=res_sb[:], in_=res[:])
             else:
                 nc.scalar.copy(out=res_sb[:], in_=res[:])
-            nc.sync.dma_start(out=out_rows[:, :, BLOCK * b0 : BLOCK * b1], in_=res_sb[:])
+            if engines == "vs":
+                for g in range(2):
+                    nc.sync.dma_start(out=out_rows[:, g, BLOCK * b0 : BLOCK * b1], in_=res_sb[:, g, :])
+            else:
+                nc.sync.dma_start(out=out_rows[:, :, BLOCK * b0 : BLOCK * b1], in_=res_sb[:])

@@ -14,6 +14,7 @@ U8 = mybir.dt.uint8
 FP8X4 = mybir.dt.float8_e4m3fn_x4
 FP4X4 = mybir.dt.float4_e2m1fn_x4
 SILU = mybir.ActivationFunctionType.Silu
+COPY = mybir.ActivationFunctionType.Copy
 
 P = 128
 PACK = 4
@@ -21,7 +22,7 @@ BLOCK = 128
 BLOCKS = V // BLOCK
 W_LOADS = (((0, 128, (0, 0)),), ((0, 128, (128, 0)),), ((0, 64, (0, 0)), (64, 128, (64, 64))))
 W_RUNS = (((0, 2048),), ((0, 2048),), ((0, 1792), (1792, 2048)))
-GATHERS = (((0, 1024),), ((0, 512), (512, 1024)), ((0, 1024),), ((0, 256), (256, 512), (512, 768), (768, 1024)))
+GATHERS = (((0, 896),), ((0, 512), (512, 1024)), ((0, 1024),), ((0, 128), (128, 320), (320, 512), (512, 768), (768, 1024)))
 OUT_STEPS = ((0, 1, "v"), (1, 2, "v"), (2, 3, "s"), (3, 4, "vs"))
 E_LOADS = ((0, 1), (1, 2), (2, 3), (3, 4))
 E_ON_SCALAR = (128, 128, 0, 0)
@@ -89,6 +90,10 @@ def tile_picked_edgeup_silu_e_kernel(tc, xT, eT, w1, w2, w3, w4_words, w4_scales
             dst = picked[side][:].rearrange("p (v u e) -> p v u e", u=2, e=2)[:, v0 - V * side : v1 - V * side, u, :]
             return dict(out=dst, in_=planes[u][:, :, v0:v1].rearrange("p e v -> p v e"))
 
+        first_row = keep.tile([P, T], BF16, name="first_row", align_bytes=256)
+        nc.scalar.copy(out=first_row[:], in_=x_raw[0][:])
+        rest = GATHERS[0][0][1]
+        nc.scalar.activation(planes[0][:, 0, rest:S], first_row[:].indirect(offsets[:, rest // 16 : S // 16]), COPY)
         for j in range(PACK):
             for v0, v1 in GATHERS[j]:
                 nc.vector.tensor_copy(out=planes[j // 2][:, j % 2, v0:v1], in_=x_raw[j][:].indirect(offsets[:, v0 // 16 : v1 // 16]))
@@ -96,7 +101,7 @@ def tile_picked_edgeup_silu_e_kernel(tc, xT, eT, w1, w2, w3, w4_words, w4_scales
                     nc.scalar.copy(**place(j // 2, v0, v1))
         x_q = [quantize("x0", picked[0][:], V)]
         targets = picked[1]
-        for v0, v1 in GATHERS[3][2:]:
+        for v0, v1 in GATHERS[3][3:]:
             nc.vector.tensor_copy(**place(1, v0, v1))
 
         def edge_codes(b):

@@ -20,12 +20,9 @@ P = 128
 PACK = 4
 BLOCK = 128
 BLOCKS = V // BLOCK
-W_LOADS = (((0, 128, (0, 0)),), ((0, 128, (128, 0)),), ((0, 64, (0, 0)), (64, 128, (64, 64))))
-W_RUNS = (((0, 2048),), ((0, 2048),), ((0, 1792), (1792, 2048)))
-GATHERS = (((0, 896),), ((0, 512), (512, 1024)), ((0, 1024),), ((0, 128), (128, 320), (320, 512), (512, 768), (768, 1024)))
-OUT_STEPS = ((0, 1, "v"), (1, 2, "v"), (2, 3, "s"), (3, 4, "vs"))
-E_LOADS = ((0, 1), (1, 2), (2, 3), (3, 4))
-E_ON_SCALAR = (128, 128, 0, 0)
+EARLY_ON_VECTOR = 512
+LAST_ON_VECTOR = 384
+W3_CUT = 64
 
 
 def tile_picked_edgeup_silu_e_kernel(tc, xT, eT, w1, w2, w3, w4_words, w4_scales, offs, out):
@@ -34,30 +31,33 @@ def tile_picked_edgeup_silu_e_kernel(tc, xT, eT, w1, w2, w3, w4_words, w4_scales
         keep = ctx.enter_context(tc.tile_pool(name="keep", bufs=1))
         psum = ctx.enter_context(tc.psum_pool(name="psum", bufs=1))
 
+        def sbuf(name, shape, dtype, tag=None):
+            return keep.tile(shape, dtype, name=name, tag=tag or name, align_bytes=256)
+
         def quantize(name, values, width, tag=None):
-            codes = keep.tile([P, width], U32, name=name + "_codes", tag=tag or name + "_codes", align_bytes=256)
-            scales = keep.tile([P, width], U8, name=name + "_scales", align_bytes=256)
+            codes = sbuf(name + "_codes", [P, width], U32, tag)
+            scales = sbuf(name + "_scales", [P, width], U8)
             nc.vector.quantize_mx(out=codes[:].bitcast(FP8X4), scales=scales[:], in_=values)
             return codes, scales
 
-        def shared_copy(dst, src, share):
-            if share > 0:
-                nc.vector.tensor_copy(out=dst[:, 0:share], in_=src[:, 0:share])
-            if share < dst.shape[1]:
-                nc.scalar.copy(out=dst[:, share:], in_=src[:, share:])
+        def copy_on(engine, dst, src):
+            if engine == "v":
+                nc.vector.tensor_copy(out=dst, in_=src)
+            else:
+                nc.scalar.copy(out=dst, in_=src)
 
         zero = keep.tile([P, 1], F32, name="zero")
         nc.vector.memset(zero[:], 0.0)
         bias = keep.tile([P, 1], F32, name="bias")
         nc.scalar.activation(bias[:], zero[:], SILU)
-        w4_s = keep.tile([P, N], U8, name="w4_s", align_bytes=256)
+        w4_s = sbuf("w4_s", [P, N], U8)
         nc.vector.memset(w4_s[:].bitcast(I32), 0)
 
         x_rows = xT.rearrange("(p j) t -> p j t", j=PACK)
-        offsets = keep.tile([P, S // 16], U16, name="offsets", align_bytes=256)
+        offsets = sbuf("offsets", [P, S // 16], U16)
         x_raw = []
         for j in range(PACK):
-            row = keep.tile([P, T], F32, name="x_raw%d" % j, align_bytes=256)
+            row = sbuf("x_raw%d" % j, [P, T], F32)
             nc.sync.dma_start(out=row[:], in_=x_rows[:, j, :])
             x_raw.append(row)
             if j == 0:
@@ -65,8 +65,9 @@ def tile_picked_edgeup_silu_e_kernel(tc, xT, eT, w1, w2, w3, w4_words, w4_scales
         w_raw = []
         for i, w in enumerate((w1, w2, w3)):
             w_runs = w.rearrange("(p j) c -> p (j c)", j=PACK)
-            raw = keep.tile([P, PACK * H], F32, name="w_raw%d" % i, tag="w_raw%d" % i, align_bytes=256)
-            for a0, a1 in W_RUNS[i]:
+            raw = sbuf("w_raw%d" % i, [P, PACK * H], F32)
+            cut = (PACK - 1) * H + PACK * W3_CUT
+            for a0, a1 in ((0, cut), (cut, PACK * H)) if i == 2 else ((0, PACK * H),):
                 nc.sync.dma_start(out=raw[:, a0:a1], in_=w_runs[:, a0:a1])
             w_raw.append(raw)
             if i == 0:
@@ -74,117 +75,110 @@ def tile_picked_edgeup_silu_e_kernel(tc, xT, eT, w1, w2, w3, w4_words, w4_scales
                     nc.sync.dma_start(out=w4_s[32 * q : 32 * q + 4, :].bitcast(I32), in_=w4_scales[0, 4 * q : 4 * q + 4, :].bitcast(I32))
         e_rows = eT.rearrange("(p j) v -> p j v", j=PACK)
         e_raw = []
-        for b0, b1 in E_LOADS:
-            raw = keep.tile([P, PACK, BLOCK * (b1 - b0)], F32, name="e_raw%d" % b0, tag="e_raw%d" % b0, align_bytes=256)
-            nc.sync.dma_start(out=raw[:], in_=e_rows[:, :, BLOCK * b0 : BLOCK * b1])
-            for b in range(b0, b1):
-                e_raw.append(raw[:, :, BLOCK * (b - b0) : BLOCK * (b - b0 + 1)])
-        w4_w = keep.tile([P, 2 * N], U8, name="w4_w", align_bytes=256)
+        for b in range(BLOCKS):
+            raw = sbuf("e_raw%d" % b, [P, PACK, BLOCK], F32)
+            nc.sync.dma_start(out=raw[:], in_=e_rows[:, :, BLOCK * b : BLOCK * (b + 1)])
+            e_raw.append(raw)
+        w4_w = sbuf("w4_w", [P, 2 * N], U8)
         nc.sync.dma_start(out=w4_w[:], in_=w4_words[0])
 
-        planes = [keep.tile([P, 2, S], BF16, name="planes%d" % u, align_bytes=256) for u in range(2)]
-        picked = [keep.tile([P, V * PACK], BF16, name="picked%d" % side, align_bytes=256) for side in range(2)]
+        planes = [sbuf("planes%d" % u, [P, 2, S], BF16) for u in range(2)]
+        picked = [sbuf("picked%d" % side, [P, V * PACK], BF16) for side in range(2)]
 
-        def place(u, v0, v1):
-            side = v0 // V
-            dst = picked[side][:].rearrange("p (v u e) -> p v u e", u=2, e=2)[:, v0 - V * side : v1 - V * side, u, :]
-            return dict(out=dst, in_=planes[u][:, :, v0:v1].rearrange("p e v -> p v e"))
+        def gather(engine, j, v0, v1):
+            dst = planes[j // 2][:, j % 2, v0:v1]
+            src = x_raw[j][:].indirect(offsets[:, v0 // 16 : v1 // 16])
+            if engine == "v":
+                nc.vector.tensor_copy(out=dst, in_=src)
+            else:
+                nc.scalar.activation(dst, src, COPY)
 
-        first_row = keep.tile([P, T], BF16, name="first_row", align_bytes=256)
-        nc.scalar.copy(out=first_row[:], in_=x_raw[0][:])
-        rest = GATHERS[0][0][1]
-        nc.scalar.activation(planes[0][:, 0, rest:S], first_row[:].indirect(offsets[:, rest // 16 : S // 16]), COPY)
-        for j in range(PACK):
-            for v0, v1 in GATHERS[j]:
-                nc.vector.tensor_copy(out=planes[j // 2][:, j % 2, v0:v1], in_=x_raw[j][:].indirect(offsets[:, v0 // 16 : v1 // 16]))
-                if j == 1 or (j == 3 and v0 < V):
-                    nc.scalar.copy(**place(j // 2, v0, v1))
-        x_q = [quantize("x0", picked[0][:], V)]
-        targets = picked[1]
-        for v0, v1 in GATHERS[3][3:]:
-            nc.vector.tensor_copy(**place(1, v0, v1))
+        def place(u, side):
+            dst = picked[side][:].rearrange("p (v u e) -> p v u e", u=2, e=2)[:, :, u, :]
+            nc.vector.tensor_copy(out=dst, in_=planes[u][:, :, V * side : V * (side + 1)].rearrange("p e v -> p v e"))
 
-        def edge_codes(b):
-            grouped = keep.tile([P, BLOCK * PACK], BF16, name="e_bf%d" % b, align_bytes=256)
-            dst = grouped[:].rearrange("p (c i j) -> p c j i", i=4, j=PACK)
-            shared_copy(dst, e_raw[b].rearrange("p j (c i) -> p c j i", i=4), (BLOCK - E_ON_SCALAR[b]) // 4)
+        for j in range(PACK - 1):
+            gather("v", j, 0, EARLY_ON_VECTOR)
+            gather("s", j, EARLY_ON_VECTOR, S)
+            if j == 1:
+                place(0, 0)
+                place(0, 1)
+        gather("v", PACK - 1, 0, LAST_ON_VECTOR)
+        gather("s", PACK - 1, LAST_ON_VECTOR, V)
+        gather("s", PACK - 1, V, S)
+        place(1, 0)
+        place(1, 1)
+        x_q = [quantize("x%d" % side, picked[side][:], V) for side in range(2)]
+
+        def round_weights(i, g, pieces):
+            half = sbuf("w_bf%d_%d" % (i, g), [P, 2 * H], BF16)
+            dst = half[:].rearrange("p (t m j) -> p m j t", t=2, j=PACK)
+            src = w_raw[i][:].rearrange("p (j m t) -> p m j t", j=PACK, t=PACK)[:, :, :, 2 * g : 2 * g + 2]
+            for engine, m0, m1 in pieces:
+                copy_on(engine, dst[:, m0:m1], src[:, m0:m1])
+            return half
+
+        def edge_codes(b, engine):
+            grouped = sbuf("e_bf%d" % b, [P, BLOCK * PACK], BF16)
+            copy_on(engine, grouped[:].rearrange("p (c i j) -> p c j i", i=4, j=PACK), e_raw[b][:].rearrange("p j (c i) -> p c j i", i=4))
             return quantize("e%d" % b, grouped[:], BLOCK)
 
-        w_q = []
-        for i in range(3):
-            halves = {}
-            for g in (1, 0) if i == 1 else (0, 1):
-                half = keep.tile([P, 2 * H], BF16, name="w_bf%d_%d" % (i, g), tag="w_bf%d_%d" % (i, g), align_bytes=256)
-                dst = half[:].rearrange("p (t m j) -> p m j t", t=2, j=PACK)
-                src = w_raw[i][:].rearrange("p (j m t) -> p m j t", j=PACK, t=PACK)[:, :, :, 2 * g : 2 * g + 2]
-                for m0, m1, shares in W_LOADS[i]:
-                    shared_copy(dst[:, m0:m1], src[:, m0:m1], shares[g])
-                halves[g] = half
-            if i == 0:
-                first = quantize("w0_0", halves[0][:], H // 2)
-                x_q.append(quantize("x1", targets[:], V, tag="w_bf0_0"))
-                w_q.append([first, quantize("w0_1", halves[1][:], H // 2)])
-            elif i == 2:
-                first = quantize("w2_0", halves[0][:], H // 2)
-                e_first = edge_codes(0)
-                w_q.append([first, quantize("w2_1", halves[1][:], H // 2, tag="e_raw0")])
-            else:
-                second = quantize("w%d_1" % i, halves[1][:], H // 2)
-                w_q.append([quantize("w%d_0" % i, halves[0][:], H // 2, tag="w_raw%d" % i), second])
+        halves = [round_weights(0, g, (("s", 0, P),)) for g in range(2)]
+        w_q = [[quantize("w0_%d" % g, halves[g][:], H // 2) for g in range(2)]]
+        second = round_weights(1, 1, (("s", 0, P),))
+        first = round_weights(1, 0, (("v", 0, P),))
+        w_q.append([quantize("w1_0", first[:], H // 2), quantize("w1_1", second[:], H // 2)])
+        halves = [round_weights(2, g, (("s", 0, W3_CUT), ("v", W3_CUT, P))) for g in range(2)]
+        first = quantize("w2_0", halves[0][:], H // 2)
+        e_first = edge_codes(0, "s")
+        w_q.append([first, quantize("w2_1", halves[1][:], H // 2, tag="e_raw0")])
 
         def w_tile(i, t):
-            per = PACK // len(w_q[i])
-            codes, scales = w_q[i][t // per]
-            cols = slice((t % per) * P, (t % per + 1) * P)
-            return codes[:, cols].bitcast(FP8X4), scales[:, cols]
+            codes, scales = w_q[i][t // 2]
+            cols = slice((t % 2) * P, (t % 2 + 1) * P)
+            return dict(lhsT=codes[:, cols].bitcast(FP8X4), lhsT_scale=scales[:, cols])
 
         acc = [psum.tile([P, PACK, BLOCK], F32, name="acc%d" % b, tag="acc%d" % b) for b in range(BLOCKS)]
 
         def node_passes(i, b):
             cols = slice(b * BLOCK, (b + 1) * BLOCK)
-            for t in (0, 1, 2, 3) if i == 0 else (2, 3, 0, 1):
-                wc, ws = w_tile(i, t)
-                nc.tensor.matmul_mx(out=acc[b][:, t, :], lhsT=wc, lhsT_scale=ws,
-                                    rhs=x_q[i][0][:, cols].bitcast(FP8X4), rhs_scale=x_q[i][1][:, cols],
-                                    start=(i == 0 and t == 0), stop=False)
+            for t in range(PACK):
+                nc.tensor.matmul_mx(out=acc[b][:, t, :], rhs=x_q[i][0][:, cols].bitcast(FP8X4), rhs_scale=x_q[i][1][:, cols],
+                                    start=(i == 0 and t == 0), stop=False, **w_tile(i, t))
 
         for b in range(BLOCKS):
             node_passes(0, b)
 
-        h_bf = keep.tile([P, V * PACK], BF16, name="h_bf", align_bytes=256)
+        h_bf = sbuf("h_bf", [P, V * PACK], BF16)
         for b in range(BLOCKS):
             node_passes(1, b)
-            ec, es = e_first if b == 0 else edge_codes(b)
+            ec, es = e_first if b == 0 else edge_codes(b, "s" if b == 1 else "v")
             for t in range(PACK):
-                wc, ws = w_tile(2, t)
-                nc.tensor.matmul_mx(out=acc[b][:, t, :], lhsT=wc, lhsT_scale=ws, rhs=ec[:].bitcast(FP8X4), rhs_scale=es[:],
-                                    start=False, stop=(t == PACK - 1))
+                nc.tensor.matmul_mx(out=acc[b][:, t, :], rhs=ec[:].bitcast(FP8X4), rhs_scale=es[:],
+                                    start=False, stop=(t == PACK - 1), **w_tile(2, t))
             hidden = h_bf[:, PACK * BLOCK * b : PACK * BLOCK * (b + 1)]
             nc.scalar.activation(hidden.rearrange("p (v t) -> p v t", t=PACK), acc[b][:].rearrange("p t v -> p v t"), SILU, bias=bias[:])
 
         out_rows = out.rearrange("(g p) v -> p g v", p=P)
-        for b0, b1, engines in OUT_STEPS:
-            width = BLOCK * (b1 - b0)
-            hc, hs = quantize("h%d" % b0, h_bf[:, PACK * BLOCK * b0 : PACK * BLOCK * b1], width)
-            res = psum.tile([P, 2, width], F32, name="res%d" % b0)
-            halves = [res[:, 0, :], res[:, 1, :]]
-            if len(engines) == 2:
-                other = psum.tile([P, width], F32, name="res_other%d" % b0, tag="acc0")
-                halves[1] = other[:]
+        for b in range(BLOCKS):
+            last = b == BLOCKS - 1
+            cols = slice(BLOCK * b, BLOCK * (b + 1))
+            hc, hs = quantize("h%d" % b, h_bf[:, PACK * BLOCK * b : PACK * BLOCK * (b + 1)], BLOCK)
+            res = psum.tile([P, 2, BLOCK], F32, name="res%d" % b)
+            parts = [res[:, 0, :], res[:, 1, :]]
+            if last:
+                other = psum.tile([P, BLOCK], F32, name="res_other", tag="acc0")
+                parts[1] = other[:]
             for g in range(2):
-                nc.tensor.matmul_mx(out=halves[g], lhsT=w4_w[:, 2 * P * g : 2 * P * (g + 1)].bitcast(FP4X4),
+                nc.tensor.matmul_mx(out=parts[g], lhsT=w4_w[:, 2 * P * g : 2 * P * (g + 1)].bitcast(FP4X4),
                                     lhsT_scale=w4_s[:, P * g : P * (g + 1)],
                                     rhs=hc[:].bitcast(FP8X4), rhs_scale=hs[:], start=True, stop=True)
-            res_sb = keep.tile([P, 2, width], F32, name="res_sb%d" % b0, align_bytes=256)
-            if engines == "vs":
-                nc.vector.tensor_copy(out=res_sb[:, 0, :], in_=halves[0])
-                nc.scalar.copy(out=res_sb[:, 1, :], in_=halves[1])
-            elif engines == "v":
-                nc.vector.tensor_copy(out=res_sb[:], in_=res[:])
-            else:
-                nc.scalar.copy(out=res_sb[:], in_=res[:])
-            if engines == "vs":
+            res_sb = sbuf("res_sb%d" % b, [P, 2, BLOCK], F32)
+            if last:
                 for g in range(2):
-                    nc.sync.dma_start(out=out_rows[:, g, BLOCK * b0 : BLOCK * b1], in_=res_sb[:, g, :])
+                    copy_on("vs"[g], res_sb[:, g, :], parts[g])
+                for g in range(2):
+                    nc.sync.dma_start(out=out_rows[:, g, cols], in_=res_sb[:, g, :])
             else:
-                nc.sync.dma_start(out=out_rows[:, :, BLOCK * b0 : BLOCK * b1], in_=res_sb[:])
+                copy_on("s" if b == 2 else "v", res_sb[:], res[:])
+                nc.sync.dma_start(out=out_rows[:, :, cols], in_=res_sb[:])

@@ -46,9 +46,9 @@ def tile_picked_edgeup_silu_e_kernel(tc, xT, eT, w1, w2, w3, w4_words, w4_scales
             else:
                 nc.scalar.copy(out=dst, in_=src)
 
-        zero = keep.tile([P, 1], F32, name="zero")
+        zero = sbuf("zero", [P, 1], F32)
         nc.vector.memset(zero[:], 0.0)
-        bias = keep.tile([P, 1], F32, name="bias")
+        bias = sbuf("bias", [P, 1], F32)
         nc.scalar.activation(bias[:], zero[:], SILU)
         w4_s = sbuf("w4_s", [P, N], U8)
         nc.vector.memset(w4_s[:].bitcast(I32), 0)
@@ -126,12 +126,13 @@ def tile_picked_edgeup_silu_e_kernel(tc, xT, eT, w1, w2, w3, w4_words, w4_scales
         halves = [round_weights(0, g, (("s", 0, P),)) for g in range(2)]
         w_q = [[quantize("w0_%d" % g, halves[g][:], H // 2) for g in range(2)]]
         second = round_weights(1, 1, (("s", 0, P),))
-        first = round_weights(1, 0, (("v", 0, P),))
-        w_q.append([quantize("w1_0", first[:], H // 2), quantize("w1_1", second[:], H // 2)])
-        halves = [round_weights(2, g, (("s", 0, W3_CUT), ("v", W3_CUT, P))) for g in range(2)]
-        first = quantize("w2_0", halves[0][:], H // 2)
+        first = round_weights(1, 0, (("v", 0, 96), ("s", 96, P)))
+        second = quantize("w1_1", second[:], H // 2)
+        w_q.append([quantize("w1_0", first[:], H // 2), second])
+        halves = [round_weights(2, 0, (("v", 0, 32), ("s", 32, W3_CUT), ("v", W3_CUT, P))),
+                  round_weights(2, 1, (("s", 0, W3_CUT), ("v", W3_CUT, P)))]
+        w_q.append([quantize("w2_%d" % g, halves[g][:], H // 2) for g in range(2)])
         e_first = edge_codes(0, "s")
-        w_q.append([first, quantize("w2_1", halves[1][:], H // 2, tag="e_raw0")])
 
         def w_tile(i, t):
             codes, scales = w_q[i][t // 2]
@@ -142,39 +143,44 @@ def tile_picked_edgeup_silu_e_kernel(tc, xT, eT, w1, w2, w3, w4_words, w4_scales
 
         def node_passes(i, b):
             cols = slice(b * BLOCK, (b + 1) * BLOCK)
-            for t in range(PACK):
-                nc.tensor.matmul_mx(out=acc[b][:, t, :], rhs=x_q[i][0][:, cols].bitcast(FP8X4), rhs_scale=x_q[i][1][:, cols],
+            codes, scales = x_q[i]
+            for t in range(PACK) if i == 0 else (2, 3, 0, 1):
+                nc.tensor.matmul_mx(out=acc[b][:, t, :], rhs=codes[:, cols].bitcast(FP8X4), rhs_scale=scales[:, cols],
                                     start=(i == 0 and t == 0), stop=False, **w_tile(i, t))
 
         for b in range(BLOCKS):
             node_passes(0, b)
 
-        h_bf = sbuf("h_bf", [P, V * PACK], BF16)
+        h_bf = [sbuf("h_bf%d" % b, [P, BLOCK * PACK], BF16) for b in range(BLOCKS)]
         for b in range(BLOCKS):
             node_passes(1, b)
-            ec, es = e_first if b == 0 else edge_codes(b, "s" if b == 1 else "v")
+            ec, es = e_first if b == 0 else edge_codes(b, "s" if b < BLOCKS - 1 else "v")
             for t in range(PACK):
                 nc.tensor.matmul_mx(out=acc[b][:, t, :], rhs=ec[:].bitcast(FP8X4), rhs_scale=es[:],
                                     start=False, stop=(t == PACK - 1), **w_tile(2, t))
-            hidden = h_bf[:, PACK * BLOCK * b : PACK * BLOCK * (b + 1)]
-            nc.scalar.activation(hidden.rearrange("p (v t) -> p v t", t=PACK), acc[b][:].rearrange("p t v -> p v t"), SILU, bias=bias[:])
+            hidden = h_bf[b][:]
+            nc.scalar.activation(hidden.rearrange("p (v t) -> p v t", t=PACK), acc[b][:].rearrange("p t v -> p v t"), SILU,
+                                 bias=(bias[:], bias[:], zero[:], 0.0)[b])
 
         out_rows = out.rearrange("(g p) v -> p g v", p=P)
-        for b in range(BLOCKS):
-            last = b == BLOCKS - 1
-            cols = slice(BLOCK * b, BLOCK * (b + 1))
-            hc, hs = quantize("h%d" % b, h_bf[:, PACK * BLOCK * b : PACK * BLOCK * (b + 1)], BLOCK)
+
+        def second_layer(b):
+            hc, hs = quantize("h%d" % b, h_bf[b][:], BLOCK)
             res = psum.tile([P, 2, BLOCK], F32, name="res%d" % b)
             parts = [res[:, 0, :], res[:, 1, :]]
-            if last:
+            if b == BLOCKS - 1:
                 other = psum.tile([P, BLOCK], F32, name="res_other", tag="acc0")
                 parts[1] = other[:]
             for g in range(2):
                 nc.tensor.matmul_mx(out=parts[g], lhsT=w4_w[:, 2 * P * g : 2 * P * (g + 1)].bitcast(FP4X4),
                                     lhsT_scale=w4_s[:, P * g : P * (g + 1)],
                                     rhs=hc[:].bitcast(FP8X4), rhs_scale=hs[:], start=True, stop=True)
-            res_sb = sbuf("res_sb%d" % b, [P, 2, BLOCK], F32)
-            if last:
+            return res, parts
+
+        def store(b, res, parts):
+            cols = slice(BLOCK * b, BLOCK * (b + 1))
+            res_sb = sbuf("res_sb%d" % b, [P, 2, BLOCK], F32, ("bias", "zero")[b] if b < 2 else None)
+            if b == BLOCKS - 1:
                 for g in range(2):
                     copy_on("vs"[g], res_sb[:, g, :], parts[g])
                 for g in range(2):
@@ -182,3 +188,9 @@ def tile_picked_edgeup_silu_e_kernel(tc, xT, eT, w1, w2, w3, w4_words, w4_scales
             else:
                 copy_on("s" if b == 2 else "v", res_sb[:], res[:])
                 nc.sync.dma_start(out=out_rows[:, :, cols], in_=res_sb[:])
+
+        results = [second_layer(0)]
+        for b in range(1, BLOCKS):
+            results.append(second_layer(b))
+            store(b - 1, *results[b - 1])
+        store(BLOCKS - 1, *results[BLOCKS - 1])

@@ -20,8 +20,7 @@ P = 128
 PACK = 4
 BLOCK = 128
 BLOCKS = V // BLOCK
-EARLY_ON_VECTOR = 512
-LAST_ON_VECTOR = 384
+ON_VECTOR = 384
 W3_CUT = 64
 
 
@@ -83,32 +82,36 @@ def tile_picked_edgeup_silu_e_kernel(tc, xT, eT, w1, w2, w3, w4_words, w4_scales
         nc.sync.dma_start(out=w4_w[:], in_=w4_words[0])
 
         planes = [sbuf("planes%d" % u, [P, 2, S], BF16) for u in range(2)]
-        picked = [sbuf("picked%d" % side, [P, V * PACK], BF16) for side in range(2)]
+        picked = sbuf("picked", [P, S * PACK], BF16)
 
-        def gather(engine, j, v0, v1):
-            dst = planes[j // 2][:, j % 2, v0:v1]
-            src = x_raw[j][:].indirect(offsets[:, v0 // 16 : v1 // 16])
-            if engine == "v":
-                nc.vector.tensor_copy(out=dst, in_=src)
-            else:
-                nc.scalar.activation(dst, src, COPY)
+        def gather_in_place(j):
+            dst = picked[:].rearrange("p (v t) -> p v t", t=PACK)[:, 0:ON_VECTOR, j]
+            nc.vector.tensor_copy(out=dst, in_=x_raw[j][:].indirect(offsets[:, 0 : ON_VECTOR // 16]))
 
-        def place(u, side):
-            dst = picked[side][:].rearrange("p (v u e) -> p v u e", u=2, e=2)[:, :, u, :]
-            nc.vector.tensor_copy(out=dst, in_=planes[u][:, :, V * side : V * (side + 1)].rearrange("p e v -> p v e"))
+        def gather_plane(j, v0, v1):
+            nc.scalar.activation(planes[j // 2][:, j % 2, v0:v1], x_raw[j][:].indirect(offsets[:, v0 // 16 : v1 // 16]), COPY)
 
+        def place(u, v0, v1):
+            dst = picked[:].rearrange("p (v u e) -> p v u e", u=2, e=2)[:, v0:v1, u, :]
+            nc.vector.tensor_copy(out=dst, in_=planes[u][:, :, v0:v1].rearrange("p e v -> p v e"))
+
+        middle = (ON_VECTOR + S) // 2
+        early = {0: ((ON_VECTOR, S),), 1: ((ON_VECTOR, middle), (middle, S)), 2: ((ON_VECTOR, S),)}
         for j in range(PACK - 1):
-            gather("v", j, 0, EARLY_ON_VECTOR)
-            gather("s", j, EARLY_ON_VECTOR, S)
-            if j == 1:
-                place(0, 0)
-                place(0, 1)
-        gather("v", PACK - 1, 0, LAST_ON_VECTOR)
-        gather("s", PACK - 1, LAST_ON_VECTOR, V)
-        gather("s", PACK - 1, V, S)
-        place(1, 0)
-        place(1, 1)
-        x_q = [quantize("x%d" % side, picked[side][:], V) for side in range(2)]
+            gather_in_place(j)
+            for v0, v1 in early[j]:
+                gather_plane(j, v0, v1)
+                if j == 1:
+                    place(0, v0, v1)
+        gather_in_place(PACK - 1)
+        last = ((ON_VECTOR, V), (V, V + V // 2), (V + V // 2, S))
+        for v0, v1 in last:
+            gather_plane(PACK - 1, v0, v1)
+        place(1, *last[0])
+        x_q = [quantize("x0", picked[:, 0 : V * PACK], V)]
+        for v0, v1 in last[1:]:
+            place(1, v0, v1)
+        x_q.append(quantize("x1", picked[:, V * PACK : S * PACK], V))
 
         def round_weights(i, g, pieces):
             half = sbuf("w_bf%d_%d" % (i, g), [P, 2 * H], BF16)
@@ -123,12 +126,11 @@ def tile_picked_edgeup_silu_e_kernel(tc, xT, eT, w1, w2, w3, w4_words, w4_scales
             copy_on(engine, grouped[:].rearrange("p (c i j) -> p c j i", i=4, j=PACK), e_raw[b][:].rearrange("p j (c i) -> p c j i", i=4))
             return quantize("e%d" % b, grouped[:], BLOCK)
 
-        halves = [round_weights(0, g, (("s", 0, P),)) for g in range(2)]
+        halves = [round_weights(0, 0, (("s", 0, P),)), round_weights(0, 1, (("s", 0, 96), ("v", 96, P)))]
         w_q = [[quantize("w0_%d" % g, halves[g][:], H // 2) for g in range(2)]]
         second = round_weights(1, 1, (("s", 0, P),))
-        first = round_weights(1, 0, (("v", 0, 96), ("s", 96, P)))
-        second = quantize("w1_1", second[:], H // 2)
-        w_q.append([quantize("w1_0", first[:], H // 2), second])
+        first = round_weights(1, 0, (("v", 0, P),))
+        w_q.append([quantize("w1_0", first[:], H // 2), quantize("w1_1", second[:], H // 2)])
         halves = [round_weights(2, 0, (("v", 0, 32), ("s", 32, W3_CUT), ("v", W3_CUT, P))),
                   round_weights(2, 1, (("s", 0, W3_CUT), ("v", W3_CUT, P)))]
         w_q.append([quantize("w2_%d" % g, halves[g][:], H // 2) for g in range(2)])
@@ -144,7 +146,7 @@ def tile_picked_edgeup_silu_e_kernel(tc, xT, eT, w1, w2, w3, w4_words, w4_scales
         def node_passes(i, b):
             cols = slice(b * BLOCK, (b + 1) * BLOCK)
             codes, scales = x_q[i]
-            for t in range(PACK) if i == 0 else (2, 3, 0, 1):
+            for t in range(PACK):
                 nc.tensor.matmul_mx(out=acc[b][:, t, :], rhs=codes[:, cols].bitcast(FP8X4), rhs_scale=scales[:, cols],
                                     start=(i == 0 and t == 0), stop=False, **w_tile(i, t))
 

@@ -113,12 +113,15 @@ def tile_picked_edgeup_silu_e_kernel(tc, xT, eT, w1, w2, w3, w4_words, w4_scales
             place(1, v0, v1)
         x_q.append(quantize("x1", picked[:, V * PACK : S * PACK], V))
 
-        def round_weights(i, g, pieces):
-            half = sbuf("w_bf%d_%d" % (i, g), [P, 2 * H], BF16)
+        def round_piece(engine, half, i, g, m0, m1):
             dst = half[:].rearrange("p (t m j) -> p m j t", t=2, j=PACK)
             src = w_raw[i][:].rearrange("p (j m t) -> p m j t", j=PACK, t=PACK)[:, :, :, 2 * g : 2 * g + 2]
+            copy_on(engine, dst[:, m0:m1], src[:, m0:m1])
+
+        def round_weights(i, g, pieces):
+            half = sbuf("w_bf%d_%d" % (i, g), [P, 2 * H], BF16)
             for engine, m0, m1 in pieces:
-                copy_on(engine, dst[:, m0:m1], src[:, m0:m1])
+                round_piece(engine, half, i, g, m0, m1)
             return half
 
         def edge_codes(b, engine):
@@ -131,8 +134,14 @@ def tile_picked_edgeup_silu_e_kernel(tc, xT, eT, w1, w2, w3, w4_words, w4_scales
         second = round_weights(1, 1, (("s", 0, P),))
         first = round_weights(1, 0, (("v", 0, P),))
         w_q.append([quantize("w1_0", first[:], H // 2), quantize("w1_1", second[:], H // 2)])
-        halves = [round_weights(2, 0, (("v", 0, 32), ("s", 32, W3_CUT), ("v", W3_CUT, P))),
-                  round_weights(2, 1, (("s", 0, W3_CUT), ("v", W3_CUT, P)))]
+        second = sbuf("w_bf2_1", [P, 2 * H], BF16)
+        first = sbuf("w_bf2_0", [P, 2 * H], BF16)
+        round_piece("v", first, 2, 0, 0, W3_CUT)
+        round_piece("s", second, 2, 1, 0, 56)
+        round_piece("v", first, 2, 0, 96, P)
+        round_piece("s", first, 2, 0, W3_CUT, 96)
+        round_piece("v", second, 2, 1, 56, P)
+        halves = [first, second]
         w_q.append([quantize("w2_%d" % g, halves[g][:], H // 2) for g in range(2)])
         e_first = edge_codes(0, "s")
 
@@ -162,7 +171,7 @@ def tile_picked_edgeup_silu_e_kernel(tc, xT, eT, w1, w2, w3, w4_words, w4_scales
                                     start=False, stop=(t == PACK - 1), **w_tile(2, t))
             hidden = h_bf[b][:]
             nc.scalar.activation(hidden.rearrange("p (v t) -> p v t", t=PACK), acc[b][:].rearrange("p t v -> p v t"), SILU,
-                                 bias=(bias[:], bias[:], zero[:], 0.0)[b])
+                                 bias=(bias if b < 2 else zero)[:])
 
         out_rows = out.rearrange("(g p) v -> p g v", p=P)
 
@@ -188,11 +197,11 @@ def tile_picked_edgeup_silu_e_kernel(tc, xT, eT, w1, w2, w3, w4_words, w4_scales
                 for g in range(2):
                     nc.sync.dma_start(out=out_rows[:, g, cols], in_=res_sb[:, g, :])
             else:
-                copy_on("s" if b == 2 else "v", res_sb[:], res[:])
+                copy_on("s" if b == 1 else "v", res_sb[:], res[:])
                 nc.sync.dma_start(out=out_rows[:, :, cols], in_=res_sb[:])
 
-        results = [second_layer(0)]
+        results = [second_layer(0), second_layer(1)]
+        store(0, *results[0])
+        results.extend(second_layer(b) for b in range(2, BLOCKS))
         for b in range(1, BLOCKS):
-            results.append(second_layer(b))
-            store(b - 1, *results[b - 1])
-        store(BLOCKS - 1, *results[BLOCKS - 1])
+            store(b, *results[b])

@@ -15,6 +15,7 @@ FP8X4 = mybir.dt.float8_e4m3fn_x4
 FP4X4 = mybir.dt.float4_e2m1fn_x4
 SILU = mybir.ActivationFunctionType.Silu
 COPY = mybir.ActivationFunctionType.Copy
+IDENTITY = mybir.ActivationFunctionType.Identity
 
 P = 128
 PACK = 4
@@ -49,6 +50,8 @@ def tile_picked_edgeup_silu_e_kernel(tc, xT, eT, w1, w2, w3, w4_words, w4_scales
         nc.vector.memset(zero[:], 0.0)
         bias = sbuf("bias", [P, 1], F32)
         nc.scalar.activation(bias[:], zero[:], SILU)
+        w1_bias = sbuf("w1_bias", [P, 1], F32)
+        nc.vector.memset(w1_bias[:], 0.0)
         w4_s = sbuf("w4_s", [P, N], U8)
         nc.vector.memset(w4_s[:].bitcast(I32), 0)
 
@@ -111,12 +114,14 @@ def tile_picked_edgeup_silu_e_kernel(tc, xT, eT, w1, w2, w3, w4_words, w4_scales
         x_q = [quantize("x0", picked[:, 0 : V * PACK], V)]
         for v0, v1 in last[1:]:
             place(1, v0, v1)
-        x_q.append(quantize("x1", picked[:, V * PACK : S * PACK], V))
 
         def round_piece(engine, half, i, g, m0, m1):
             dst = half[:].rearrange("p (t m j) -> p m j t", t=2, j=PACK)
             src = w_raw[i][:].rearrange("p (j m t) -> p m j t", j=PACK, t=PACK)[:, :, :, 2 * g : 2 * g + 2]
-            copy_on(engine, dst[:, m0:m1], src[:, m0:m1])
+            if (i, g) == (0, 0):
+                nc.scalar.activation(dst[:, m0:m1], src[:, m0:m1], IDENTITY, bias=w1_bias[:])
+            else:
+                copy_on(engine, dst[:, m0:m1], src[:, m0:m1])
 
         def round_weights(i, g, pieces):
             half = sbuf("w_bf%d_%d" % (i, g), [P, 2 * H], BF16)
@@ -130,10 +135,13 @@ def tile_picked_edgeup_silu_e_kernel(tc, xT, eT, w1, w2, w3, w4_words, w4_scales
             return quantize("e%d" % b, grouped[:], BLOCK)
 
         halves = [round_weights(0, 0, (("s", 0, P),)), round_weights(0, 1, (("s", 0, 96), ("v", 96, P)))]
-        w_q = [[quantize("w0_%d" % g, halves[g][:], H // 2) for g in range(2)]]
+        first = quantize("w0_0", halves[0][:], H // 2)
+        x_q.append(quantize("x1", picked[:, V * PACK : S * PACK], V, "w1_bias"))
+        w_q = [[first, quantize("w0_1", halves[1][:], H // 2)]]
         second = round_weights(1, 1, (("s", 0, P),))
         first = round_weights(1, 0, (("v", 0, P),))
-        w_q.append([quantize("w1_0", first[:], H // 2), quantize("w1_1", second[:], H // 2)])
+        second = quantize("w1_1", second[:], H // 2)
+        w_q.append([quantize("w1_0", first[:], H // 2, "w_raw1"), second])
         second = sbuf("w_bf2_1", [P, 2 * H], BF16)
         first = sbuf("w_bf2_0", [P, 2 * H], BF16)
         round_piece("v", first, 2, 0, 0, W3_CUT)
@@ -155,7 +163,7 @@ def tile_picked_edgeup_silu_e_kernel(tc, xT, eT, w1, w2, w3, w4_words, w4_scales
         def node_passes(i, b):
             cols = slice(b * BLOCK, (b + 1) * BLOCK)
             codes, scales = x_q[i]
-            for t in range(PACK):
+            for t in range(PACK) if i == 0 else (2, 3, 0, 1):
                 nc.tensor.matmul_mx(out=acc[b][:, t, :], rhs=codes[:, cols].bitcast(FP8X4), rhs_scale=scales[:, cols],
                                     start=(i == 0 and t == 0), stop=False, **w_tile(i, t))
 

@@ -21,7 +21,7 @@ P = 128
 PACK = 4
 BLOCK = 128
 BLOCKS = V // BLOCK
-ON_VECTOR = 384
+ON_VECTOR = (384, 384, 256, 256)
 W3_CUT = 64
 
 
@@ -88,8 +88,8 @@ def tile_picked_edgeup_silu_e_kernel(tc, xT, eT, w1, w2, w3, w4_words, w4_scales
         picked = sbuf("picked", [P, S * PACK], BF16)
 
         def gather_in_place(j):
-            dst = picked[:].rearrange("p (v t) -> p v t", t=PACK)[:, 0:ON_VECTOR, j]
-            nc.vector.tensor_copy(out=dst, in_=x_raw[j][:].indirect(offsets[:, 0 : ON_VECTOR // 16]))
+            dst = picked[:].rearrange("p (v t) -> p v t", t=PACK)[:, 0 : ON_VECTOR[j], j]
+            nc.vector.tensor_copy(out=dst, in_=x_raw[j][:].indirect(offsets[:, 0 : ON_VECTOR[j] // 16]))
 
         def gather_plane(j, v0, v1):
             nc.scalar.activation(planes[j // 2][:, j % 2, v0:v1], x_raw[j][:].indirect(offsets[:, v0 // 16 : v1 // 16]), COPY)
@@ -98,8 +98,8 @@ def tile_picked_edgeup_silu_e_kernel(tc, xT, eT, w1, w2, w3, w4_words, w4_scales
             dst = picked[:].rearrange("p (v u e) -> p v u e", u=2, e=2)[:, v0:v1, u, :]
             nc.vector.tensor_copy(out=dst, in_=planes[u][:, :, v0:v1].rearrange("p e v -> p v e"))
 
-        middle = (ON_VECTOR + S) // 2
-        early = {0: ((ON_VECTOR, S),), 1: ((ON_VECTOR, middle), (middle, S)), 2: ((ON_VECTOR, S),)}
+        middle = (ON_VECTOR[1] + S) // 2
+        early = {0: ((ON_VECTOR[0], S),), 1: ((ON_VECTOR[1], middle), (middle, S)), 2: ((ON_VECTOR[2], S),)}
         for j in range(PACK - 1):
             gather_in_place(j)
             for v0, v1 in early[j]:
@@ -107,7 +107,7 @@ def tile_picked_edgeup_silu_e_kernel(tc, xT, eT, w1, w2, w3, w4_words, w4_scales
                 if j == 1:
                     place(0, v0, v1)
         gather_in_place(PACK - 1)
-        last = ((ON_VECTOR, V), (V, V + V // 2), (V + V // 2, S))
+        last = ((ON_VECTOR[3], V), (V, V + V // 2), (V + V // 2, S))
         for v0, v1 in last:
             gather_plane(PACK - 1, v0, v1)
         place(1, *last[0])

@@ -77,12 +77,6 @@ def tile_picked_edgeup_silu_e_kernel(tc, xT, eT, w1, w2, w3, w4_words, w4_scales
                     nc.sync.dma_start(out=w4_s[32 * q : 32 * q + 4, :].bitcast(I32), in_=w4_scales[0, 4 * q : 4 * q + 4, :].bitcast(I32))
         e_rows = eT.rearrange("(p j) v -> p j v", j=PACK)
         e_raw = []
-        for b in range(BLOCKS):
-            raw = sbuf("e_raw%d" % b, [P, PACK, BLOCK], F32)
-            nc.sync.dma_start(out=raw[:], in_=e_rows[:, :, BLOCK * b : BLOCK * (b + 1)])
-            e_raw.append(raw)
-        w4_w = sbuf("w4_w", [P, 2 * N], U8)
-        nc.sync.dma_start(out=w4_w[:], in_=w4_words[0])
 
         planes = [sbuf("planes%d" % u, [P, 2, S], BF16) for u in range(2)]
         picked = sbuf("picked", [P, S * PACK], BF16)
@@ -131,13 +125,19 @@ def tile_picked_edgeup_silu_e_kernel(tc, xT, eT, w1, w2, w3, w4_words, w4_scales
 
         def edge_codes(b, engine):
             grouped = sbuf("e_bf%d" % b, [P, BLOCK * PACK], BF16)
-            copy_on(engine, grouped[:].rearrange("p (c i j) -> p c j i", i=4, j=PACK), e_raw[b][:].rearrange("p j (c i) -> p c j i", i=4))
+            copy_on(engine, grouped[:].rearrange("p (c i j) -> p c j i", i=4, j=PACK), e_raw[b].rearrange("p j (c i) -> p c j i", i=4))
             return quantize("e%d" % b, grouped[:], BLOCK)
 
         halves = [round_weights(0, 0, (("s", 0, P),)), round_weights(0, 1, (("s", 0, 96), ("v", 96, P)))]
         first = quantize("w0_0", halves[0][:], H // 2)
         x_q.append(quantize("x1", picked[:, V * PACK : S * PACK], V, "w1_bias"))
         w_q = [[first, quantize("w0_1", halves[1][:], H // 2)]]
+        e_all = sbuf("e_all", [P, BLOCKS, PACK, BLOCK], F32, "w_raw0")
+        for b in range(BLOCKS):
+            nc.sync.dma_start(out=e_all[:, b], in_=e_rows[:, :, BLOCK * b : BLOCK * (b + 1)])
+            e_raw.append(e_all[:, b])
+        w4_w = sbuf("w4_w", [P, 2 * N], U8, "w_bf0_1")
+        nc.sync.dma_start(out=w4_w[:], in_=w4_words[0])
         second = round_weights(1, 1, (("s", 0, P),))
         first = round_weights(1, 0, (("v", 0, P),))
         second = quantize("w1_1", second[:], H // 2)

from contextlib import ExitStack

import concourse.mybir as mybir

K, T, S, V, H, N = 512, 2048, 1024, 512, 512, 256
FLOPS = 2 * V * (3 * K * H + H * N)

F32 = mybir.dt.float32
BF16 = mybir.dt.bfloat16
U32 = mybir.dt.uint32
I32 = mybir.dt.int32
U16 = mybir.dt.uint16
U8 = mybir.dt.uint8
FP8X4 = mybir.dt.float8_e4m3fn_x4
FP4X4 = mybir.dt.float4_e2m1fn_x4
SILU = mybir.ActivationFunctionType.Silu
COPY = mybir.ActivationFunctionType.Copy
IDENTITY = mybir.ActivationFunctionType.Identity

P = 128
PACK = 4
BLOCK = 128
BLOCKS = V // BLOCK
ON_VECTOR = (384, 384, 256, 256)
W3_CUT = 64


def tile_picked_edgeup_silu_e_kernel(tc, xT, eT, w1, w2, w3, w4_words, w4_scales, offs, out):
    nc = tc.nc
    with ExitStack() as ctx:
        keep = ctx.enter_context(tc.tile_pool(name="keep", bufs=1))
        psum = ctx.enter_context(tc.psum_pool(name="psum", bufs=1))

        def sbuf(name, shape, dtype, tag=None):
            return keep.tile(shape, dtype, name=name, tag=tag or name, align_bytes=256)

        def quantize(name, values, width, tag=None):
            codes = sbuf(name + "_codes", [P, width], U32, tag)
            scales = sbuf(name + "_scales", [P, width], U8)
            nc.vector.quantize_mx(out=codes[:].bitcast(FP8X4), scales=scales[:], in_=values)
            return codes, scales

        def copy_on(engine, dst, src):
            if engine == "v":
                nc.vector.tensor_copy(out=dst, in_=src)
            else:
                nc.scalar.copy(out=dst, in_=src)

        zero = sbuf("zero", [P, 1], F32)
        nc.vector.memset(zero[:], 0.0)
        bias = sbuf("bias", [P, 1], F32)
        nc.scalar.activation(bias[:], zero[:], SILU)
        w1_bias = sbuf("w1_bias", [P, 1], F32)
        nc.vector.memset(w1_bias[:], 0.0)
        w4_s = sbuf("w4_s", [P, N], U8)
        nc.vector.memset(w4_s[:].bitcast(I32), 0)

        x_rows = xT.rearrange("(p j) t -> p j t", j=PACK)
        offsets = sbuf("offsets", [P, S // 16], U16)
        x_raw = []
        for j in range(PACK):
            row = sbuf("x_raw%d" % j, [P, T], F32)
            nc.sync.dma_start(out=row[:], in_=x_rows[:, j, :])
            x_raw.append(row)
            if j == 0:
                nc.sync.dma_start(offsets[:], offs)
        w_raw = []
        for i, w in enumerate((w1, w2, w3)):
            w_runs = w.rearrange("(p j) c -> p (j c)", j=PACK)
            raw = sbuf("w_raw%d" % i, [P, PACK * H], F32)
            cut = (PACK - 1) * H + PACK * W3_CUT
            for a0, a1 in ((0, cut), (cut, PACK * H)) if i == 2 else ((0, PACK * H),):
                nc.sync.dma_start(out=raw[:, a0:a1], in_=w_runs[:, a0:a1])
            w_raw.append(raw)
            if i == 0:
                for q in range(4):
                    nc.sync.dma_start(out=w4_s[32 * q : 32 * q + 4, :].bitcast(I32), in_=w4_scales[0, 4 * q : 4 * q + 4, :].bitcast(I32))
        e_rows = eT.rearrange("(p j) v -> p j v", j=PACK)
        e_raw = []

        planes = [sbuf("planes%d" % u, [P, 2, S], BF16) for u in range(2)]
        picked = sbuf("picked", [P, S * PACK], BF16)

        def gather_in_place(j):
            dst = picked[:].rearrange("p (v t) -> p v t", t=PACK)[:, 0 : ON_VECTOR[j], j]
            nc.vector.tensor_copy(out=dst, in_=x_raw[j][:].indirect(offsets[:, 0 : ON_VECTOR[j] // 16]))

        def gather_plane(j, v0, v1):
            nc.scalar.activation(planes[j // 2][:, j % 2, v0:v1], x_raw[j][:].indirect(offsets[:, v0 // 16 : v1 // 16]), COPY)

        def place(u, v0, v1):
            dst = picked[:].rearrange("p (v u e) -> p v u e", u=2, e=2)[:, v0:v1, u, :]
            nc.vector.tensor_copy(out=dst, in_=planes[u][:, :, v0:v1].rearrange("p e v -> p v e"))

        middle = (ON_VECTOR[1] + S) // 2
        early = {0: ((ON_VECTOR[0], S),), 1: ((ON_VECTOR[1], middle), (middle, S)), 2: ((ON_VECTOR[2], S),)}
        for j in range(PACK - 1):
            gather_in_place(j)
            for v0, v1 in early[j]:
                gather_plane(j, v0, v1)
                if j == 1:
                    place(0, v0, v1)
        gather_in_place(PACK - 1)
        last = ((ON_VECTOR[3], V), (V, V + V // 2), (V + V // 2, S))
        for v0, v1 in last:
            gather_plane(PACK - 1, v0, v1)
        place(1, *last[0])
        x_q = [quantize("x0", picked[:, 0 : V * PACK], V)]
        for v0, v1 in last[1:]:
            place(1, v0, v1)

        def round_piece(engine, half, i, g, m0, m1):
            dst = half[:].rearrange("p (t m j) -> p m j t", t=2, j=PACK)
            src = w_raw[i][:].rearrange("p (j m t) -> p m j t", j=PACK, t=PACK)[:, :, :, 2 * g : 2 * g + 2]
            if (i, g) == (0, 0):
                nc.scalar.activation(dst[:, m0:m1], src[:, m0:m1], IDENTITY, bias=w1_bias[:])
            else:
                copy_on(engine, dst[:, m0:m1], src[:, m0:m1])

        def round_weights(i, g, pieces):
            half = sbuf("w_bf%d_%d" % (i, g), [P, 2 * H], BF16)
            for engine, m0, m1 in pieces:
                round_piece(engine, half, i, g, m0, m1)
            return half

        def edge_codes(b, engine):
            grouped = sbuf("e_bf%d" % b, [P, BLOCK * PACK], BF16)
            copy_on(engine, grouped[:].rearrange("p (c i j) -> p c j i", i=4, j=PACK), e_raw[b].rearrange("p j (c i) -> p c j i", i=4))
            return quantize("e%d" % b, grouped[:], BLOCK)

        halves = [round_weights(0, 0, (("s", 0, P),)), round_weights(0, 1, (("s", 0, 96), ("v", 96, P)))]
        first = quantize("w0_0", halves[0][:], H // 2)
        x_q.append(quantize("x1", picked[:, V * PACK : S * PACK], V, "w1_bias"))
        w_q = [[first, quantize("w0_1", halves[1][:], H // 2)]]
        e_all = sbuf("e_all", [P, BLOCKS, PACK, BLOCK], F32, "w_raw0")
        for b in range(BLOCKS):
            nc.sync.dma_start(out=e_all[:, b], in_=e_rows[:, :, BLOCK * b : BLOCK * (b + 1)])
            e_raw.append(e_all[:, b])
        w4_w = sbuf("w4_w", [P, 2 * N], U8, "w_bf0_1")
        nc.sync.dma_start(out=w4_w[:], in_=w4_words[0])
        second = round_weights(1, 1, (("s", 0, P),))
        first = round_weights(1, 0, (("v", 0, P),))
        second = quantize("w1_1", second[:], H // 2)
        w_q.append([quantize("w1_0", first[:], H // 2, "w_raw1"), second])
        second = sbuf("w_bf2_1", [P, 2 * H], BF16)
        first = sbuf("w_bf2_0", [P, 2 * H], BF16)
        round_piece("v", first, 2, 0, 0, W3_CUT)
        round_piece("s", second, 2, 1, 0, 56)
        round_piece("v", first, 2, 0, 96, P)
        round_piece("s", first, 2, 0, W3_CUT, 96)
        round_piece("v", second, 2, 1, 56, P)
        halves = [first, second]
        w_q.append([quantize("w2_%d" % g, halves[g][:], H // 2) for g in range(2)])
        e_first = edge_codes(0, "s")

        def w_tile(i, t):
            codes, scales = w_q[i][t // 2]
            cols = slice((t % 2) * P, (t % 2 + 1) * P)
            return dict(lhsT=codes[:, cols].bitcast(FP8X4), lhsT_scale=scales[:, cols])

        acc = [psum.tile([P, PACK, BLOCK], F32, name="acc%d" % b, tag="acc%d" % b) for b in range(BLOCKS)]

        def node_passes(i, b):
            cols = slice(b * BLOCK, (b + 1) * BLOCK)
            codes, scales = x_q[i]
            for t in range(PACK) if i == 0 else (2, 3, 0, 1):
                nc.tensor.matmul_mx(out=acc[b][:, t, :], rhs=codes[:, cols].bitcast(FP8X4), rhs_scale=scales[:, cols],
                                    start=(i == 0 and t == 0), stop=False, **w_tile(i, t))

        for b in range(BLOCKS):
            node_passes(0, b)

        h_bf = [sbuf("h_bf%d" % b, [P, BLOCK * PACK], BF16) for b in range(BLOCKS)]
        for b in range(BLOCKS):
            node_passes(1, b)
            ec, es = e_first if b == 0 else edge_codes(b, "s" if b < BLOCKS - 1 else "v")
            for t in range(PACK):
                nc.tensor.matmul_mx(out=acc[b][:, t, :], rhs=ec[:].bitcast(FP8X4), rhs_scale=es[:],
                                    start=False, stop=(t == PACK - 1), **w_tile(2, t))
            hidden = h_bf[b][:]
            nc.scalar.activation(hidden.rearrange("p (v t) -> p v t", t=PACK), acc[b][:].rearrange("p t v -> p v t"), SILU,
                                 bias=(bias if b < 2 else zero)[:])

        out_rows = out.rearrange("(g p) v -> p g v", p=P)

        def second_layer(b):
            hc, hs = quantize("h%d" % b, h_bf[b][:], BLOCK)
            res = psum.tile([P, 2, BLOCK], F32, name="res%d" % b)
            parts = [res[:, 0, :], res[:, 1, :]]
            if b == BLOCKS - 1:
                other = psum.tile([P, BLOCK], F32, name="res_other", tag="acc0")
                parts[1] = other[:]
            for g in range(2):
                nc.tensor.matmul_mx(out=parts[g], lhsT=w4_w[:, 2 * P * g : 2 * P * (g + 1)].bitcast(FP4X4),
                                    lhsT_scale=w4_s[:, P * g : P * (g + 1)],
                                    rhs=hc[:].bitcast(FP8X4), rhs_scale=hs[:], start=True, stop=True)
            return res, parts

        def store(b, res, parts):
            cols = slice(BLOCK * b, BLOCK * (b + 1))
            res_sb = sbuf("res_sb%d" % b, [P, 2, BLOCK], F32, ("bias", "zero")[b] if b < 2 else None)
            if b == BLOCKS - 1:
                for g in range(2):
                    copy_on("vs"[g], res_sb[:, g, :], parts[g])
                for g in range(2):
                    nc.sync.dma_start(out=out_rows[:, g, cols], in_=res_sb[:, g, :])
            else:
                copy_on("s" if b == 1 else "v", res_sb[:], res[:])
                nc.sync.dma_start(out=out_rows[:, :, cols], in_=res_sb[:])

        results = [second_layer(0), second_layer(1)]
        store(0, *results[0])
        results.extend(second_layer(b) for b in range(2, BLOCKS))
        for b in range(1, BLOCKS):
            store(b, *results[b])
